import numpy as np, ml_dtypes
CORES = [242,247,114,119]
N = 4
BF = ml_dtypes.bfloat16
def gentries(a):
    return np.ascontiguousarray(a.reshape(8, 16, -1).transpose(0, 2, 1)).reshape(8, -1)
def gtable(e):
    e = np.asarray(e); return np.ascontiguousarray(e.reshape(8, -1, 16).transpose(0, 2, 1)).reshape(128, -1).astype(np.int32)
W, UN, P, SH, MS = 4096, 128, 32, 6, (2, 1)
def parts(rng):
    e = (0.5 + 2.5 * rng.random((N, 8, 16, 1))).astype(np.float32)
    sh = np.minimum(np.floor(256 * rng.random((N, 8, 16, W), dtype=np.float32) ** e), 255)
    return sh, rng.integers(0, W, (N, 8, UN, P))
def pack(sh, un):
    return {"shelf": np.ascontiguousarray(sh.reshape(N, 128, W)).astype(np.float32).astype(BF), "units": np.stack([gtable(a.reshape(8, -1)) for a in un])}
def setup_inputs(rng):
    sh, un = parts(rng)
    return pack(sh, un)
def setup_inputs_ties(rng):
    sh, un = parts(rng)
    sh = (rng.random((N, 8, 16, W)) < 0.03) * rng.choice(np.array([1, 7, 255]), (1, 8, 1, 1))
    sh[:, rng.integers(0, 8)] = 9
    return pack(sh, un)
def setup_inputs_alike(rng):
    sh, un = parts(rng)
    un[:, 0] = un[0, 0].copy()
    un[:, 1] = rng.choice(np.array([0, 1, W - 1, W // 2]), (N, UN, P))
    un[:, 2] = un[:, 2, :1].copy()
    un[:, 3] = un[:, 3, :, :1].copy()
    un[:, 4] = 0
    un[:, 5, 1::2] = un[:, 5, ::2].copy()
    un[:, 6, :, P // 2:] = un[:1, 6, :1, P // 2:].copy()
    return pack(sh, un)
def setup_inputs_ends(rng):
    sh, un = parts(rng)
    sh[:, :7] = sh[:1, :7].copy(); x = rng.integers(1, W, (N, 7, UN)); un[:, :7] = 0
    for g, e in enumerate((0, P - 1, P // 2 - 1, P // 2, 1, P - 2, int(rng.integers(0, P)))): un[:, g, :, e] = x[:, g]
    return pack(sh, un)
def setup_inputs_rare(rng):
    sh, un = parts(rng)
    few = W // (8 * P) * np.array([1, 2, 3, 4, 2, 3])[:, None, None]
    hit = np.argsort(rng.random((N, 6, 1, W)), axis=-1) < few
    v = rng.integers(1, 256, (N, 6, 16, W)); v[:, 0] = 1; v[:, 1] = 255
    v = np.where(hit, v, 0); v[:, 4:] = 255 - v[:, 4:]
    sh[:, :6] = v
    sh[:, 6] = rng.choice(np.array([0, 1, 2, 253, 254, 255]), (N, 16, W))
    sh[:, 7] = np.clip(rng.integers(-64, 320, (N, 16, W)), 0, 255)
    sh = np.where((sh == 0) & (rng.random(sh.shape, dtype=np.float32) < 0.5), np.float32(-0.0), sh)
    return pack(sh, un)
def setup_inputs_spread(rng):
    sh, un = parts(rng)
    k = np.exp2(8 * rng.random((N, 8, 1, W))) * (rng.random((N, 8, 1, W)) > 0.0625)
    sh = np.minimum(np.floor(rng.random((N, 8, 16, W)) * k), 255)
    un = np.minimum((W * rng.random((N, 8, UN, P)) ** rng.choice(np.array([1, 2, 4, 8]), (N, 8, 1, 1))).astype(np.int64), W - 1)
    return pack(sh, un)
def check_inputs(d):
    bad = []; v = np.asarray(d["shelf"]).astype(np.float32)
    if not np.all((v >= 0) & (v <= 255) & (v == np.floor(v))): bad.append("values of shelf")
    if np.min(d["units"]) < 0 or np.max(d["units"]) > W - 1: bad.append("range of units")
    return bad
def reference(shelf, units):
    tab = np.ascontiguousarray(shelf.astype(np.float32).astype(np.int16).reshape(N, 8, 16, W).transpose(0, 1, 3, 2))
    un = np.stack([gentries(a) for a in units]).astype(np.int64).reshape(N, 8, UN, P)
    A = np.zeros((N, 8), np.int64); rank = np.arange(N); place = np.arange(P)
    n3, g3 = rank[:, None, None], np.arange(8)[None, :, None]
    def measure(x):
        z = (A[:, :, None, None] + np.add.accumulate(x, axis=3)) & 4095
        c = ((z * z >> SH) + x) & (W - 1)
        b = tab[n3[..., None], g3[..., None], c]
        return np.sum((np.max(b, axis=3) - np.min(b, axis=3)).astype(np.int64), axis=3)
    for m in MS:
        mate = rank ^ m; low = (rank < mate)[:, None, None]
        q = measure(un)
        order = np.argsort(np.where(low, -q, q), axis=2, kind="stable")
        own = un[n3, g3, order]; qo = q[n3, g3, order]; far = own[mate]; qf = qo[mate]
        s0 = np.where(low, qo > qf, qf > qo)
        first = np.zeros((N, 8, UN), np.int64); n = P
        while n > 1:
            n = n // 2
            swapped = (place >= first[..., None]) & (place < first[..., None] + n)
            a = measure(np.where(swapped, far, own)); b = a[mate]
            s = np.where(low, a > b, b > a)
            first = np.where(s != s0, first, first + n)
        takes = np.where(low, qo < qf, qo <= qf)
        new = np.where(takes[..., None] & (place == first[..., None]), far, own)
        un = np.zeros_like(un); un[n3, g3, order] = new
        A = np.sum(first, axis=2)
    return {"yu": np.stack([gtable(a.reshape(8, -1)) for a in un]).astype(np.float32), "yq": q.astype(np.float32)}

@@ -1,0 +1,538 @@
+from concourse.bass import DstId, RemoteDMATransfer
+from concourse.mybir import dt, AluOpType as OP, AxisListType, ActivationFunctionType as AF
+
+NC, CU = 4, 32
+US = 28
+BIG = 786432.0
+HS = (16, 8, 4, 2, 1)
+SFROM = 5
+GR, VF, SFX, PEC, WAKE = 1.56, 12.0, 65.0, 0.71, 90.0
+BUCKET, LANEB, GALA, SCLA = 100.0, 1000.0, 400.0, 0.0
+BIAS = {"y": 1000.0, "sq": 1000.0, "t": 1000.0, "sf": 1000.0, "of": 1000.0, "x": 1000.0, "mk": 1000.0, "md": 1000.0, "sp": 1000.0,
+        "mn": 500.0, "vk": -2000.0, "ga": 1000.0}
+
+F32M = ["mrow", "sm", "im", "idf", "le", "same", "pm0", "pm1", "dm0", "dm1", "e1", "e2"]
+B16M = (["ineg", "i64b", "m16", "sameb", "ones", "sdp0", "sdn0", "sdp1", "sdn1", "lp0", "lp1", "ln0", "ln1"] + ["idh%d" % h for h in HS]
+        + ["dg%d" % t for t in range(1, 6)] + ["lk%d" % s for s in range(8)] + ["ql%d" % q for q in range(4)])
+H16M = ["tri", "onesb", "i64h"]
+COLF = ["pcf", "ps", "pi", "b1", "b2", "nb1", "nb2", "asum", "lam0", "lam1", "px0", "px1", "psx0", "psx1", "th0", "th1", "nl0", "nl1",
+        "va", "vb", "vv", "vt", "colr", "fc", "scl2", "ad0", "ad1", "scl1", "ad2"] + ["dc%d" % t for t in range(1, 6)]
+COLI = ["pc", "psi", "ii", "odd", "bit0", "bit1"] + ["fi%d" % h for h in (8, 4, 2, 1)]
+SCRATCH = {"cc": ("sbuf", [128, 8, 128], "bfloat16"), "st": ("dram", [512, 1024], "bfloat16"), "su": ("dram", [512, 64], "int32"),
+           "lsh": ("dram", [512, 1024], "bfloat16"), "lu": ("dram", [512, 64], "int32")}
+for _d, _l in (("float32", (("kf", 128 * len(F32M)), ("cf", len(COLF)), ("row8", 8), ("ind", 8), ("r2t", 8), ("r2f", 8), ("sq", 256), ("md", 256),
+                            ("pf", 128), ("nw", 256), ("kc", 8), ("src", 384), ("win", 384), ("ou", 256), ("sto", 256), ("lr", 256), ("yo", 256),
+                            ("lq", 512))),
+               ("bfloat16", (("kb", 128 * len(B16M)), ("r1", 4), ("r2", 8), ("negv", 512), ("cl", 128), ("cr", 128), ("mmx", 1024), ("mmn", 1024),
+                             ("sh0", 4096), ("shs", 4096), ("y", 256), ("ga", 4096), ("mx", 4096), ("mn", 4096), ("mk", 256), ("sp", 1280),
+                             ("sg", 256), ("nt", 256), ("dd", 128), ("dl", 512))),
+               ("float16", (("kh", 128 * len(H16M)), ("xo", 256), ("x", 256))),
+               ("int32", (("ci", len(COLI)), ("un0", 256), ("uns", 256), ("t3", 256), ("sf", 256))),
+               ("uint16", (("of", 256), ("po", 24)))):
+    for _n, _w in _l:
+        SCRATCH[_n] = ("sbuf", [128, _w], _d)
+for _i in range(4):
+    SCRATCH["pa%d" % _i] = ("psum", [128, 512], "float32")
+    SCRATCH["pb%d" % _i] = ("psum", [128, 512], "float32")
+LANE = "pw px y py sq t sf of ga gv mx mn pd sp pg pc mk md x pD sg nt nw fs pf dd".split()
+ONE = "vk gk srcu xo pkc kc pkr0 pkr1 pkr3 cv cs pq sq_ pl po scat red un1 un2 dst dsu dun dsh dut douq dou au ad aq loc".split()
+SEMAPHORES = [s + str(c) for s in LANE for c in range(NC)] + ONE + [s + str(q) for s in ("ash", "bs", "al") for q in range(4)]
+
+
+def vd(n, rate=1.0):
+    return max(64.0, n * rate) * 0.83 + VF
+
+
+def sd(n, rate=1.0):
+    return max(64.0, n * rate) * 0.83 + SFX
+
+
+def pe(n):
+    return n * (64 * PEC) + 10.0
+
+
+def rank_program(g, core, T, topo):
+    r = T.rank_of(core)
+    if r is None:
+        return
+    cores = list(T.cores)
+    others = [q for q in range(4) if q != r]
+    V, S, P = g.vector, g.scalar, g.tensor
+    tasks, lastw, readers, bank, count = [], {}, {}, {}, {}
+
+    def add(eng, sem, fn, reads=(), writes=(), banks=(), dur=60.0, lat=0.0, n=1, inc=1, ready=0.0, extra=()):
+        i = len(tasks)
+        deps, soft = set(extra), set()
+        for k in list(reads) + list(writes):
+            if k in lastw:
+                deps.add(lastw[k])
+        for k in writes:
+            deps.update(readers.get(k, ()))
+        for b in banks:
+            st = bank.setdefault(b, {})
+            for e in [e for e in st if e != eng]:
+                deps.update(st.pop(e))
+            if eng in st:
+                soft.add(st[eng][-1])
+            st.setdefault(eng, []).append(i)
+        for k in reads:
+            readers.setdefault(k, []).append(i)
+        for k in writes:
+            lastw[k] = i
+            readers[k] = []
+        count[sem] = count.get(sem, 0) + n * inc
+        tasks.append(dict(eng=eng, sem=sem, val=count[sem], inc=inc, fn=fn, deps=deps, soft=soft - deps, dur=dur, lat=lat, ready=ready))
+        return i
+
+    def mats(buf, names):
+        return {n: buf[:, 128 * i:128 * i + 128] for i, n in enumerate(names)}
+    kf, kb, kh = mats(T.kf, F32M), mats(T.kb, B16M), mats(T.kh, H16M)
+    cf = {n: T.cf[:, i:i + 1] for i, n in enumerate(COLF)}
+    ci = {n: T.ci[:, i:i + 1] for i, n in enumerate(COLI)}
+    ob = B16M.index("ones") * 128
+    ones1, onesrow, ones8 = T.kb[:, ob:ob + 1], T.kb[0:1, ob:ob + 128], T.kb[0:1, ob:ob + 8]
+
+    def rows(q):
+        return slice(32 * q, 32 * q + 32)
+
+    def big(q):
+        return slice(128 * q, 128 * q + 128)
+    add("S", "dun", lambda: [S.dma_start(T.un0[:, :], T.units[:, :])], (), ["un0"], dur=100, lat=2000, inc=16)
+    add("Y", "dst", lambda: [g.sync.dma_start(T.st[big(q), :], T.shelf[rows(q), :]) for q in others], (), ["st"], dur=300, lat=4000, n=3, inc=16)
+    add("S", "dsu", lambda: [S.dma_start(T.su[big(q), :], T.units[rows(q), :]) for q in others], (), ["su"], dur=300, lat=2000, n=3, inc=16)
+    add("Y", "dsh", lambda: [g.sync.dma_start(T.sh0[:, :], T.shelf[:, :])], (), ["sh0"], dur=100, lat=6000, inc=16)
+    add("Y", "bs%d" % r, lambda: [g.sync.dma_start(T.shs[rows(r), :], T.shelf[rows(r), :])], (), ["shs%d" % r], dur=100, lat=7000, inc=16)
+
+    def split(p):
+        oth = [q for q in range(4) if q != p]
+        away = [q for q in oth if (topo.host(cores[q]), topo.chip(cores[q])) != (topo.host(cores[p]), topo.chip(cores[p]))]
+        offe = topo.engines(cores[p], cores[away[0]])
+        w = len(offe) // len(away)
+        res = {q: offe[k * w:k * w + w] for k, q in enumerate(away)}
+        for q in oth:
+            if q not in away:
+                res[q] = [e for e in topo.engines(cores[p], cores[q]) if e not in offe]
+        return res, away
+    eng_of, off = split(r)
+    near = [q for q in others if q not in off]
+
+    def send(reads, src_of, dst, sem, lat):
+        def fn():
+            tr = []
+            for q in others:
+                rid, pid = topo.addr(cores[q], core)
+                tr.append(RemoteDMATransfer(dst_ids=[DstId(rid=rid, pnc=pid)], dma_engine_mask=sum(1 << e for e in eng_of[q]),
+                                            remote_sem=T.sem[sem], src=src_of(q), dst=dst))
+            g.remote_dma_fused(tr, local_sem=T.sem["loc"])
+            return []
+        add("G", "loc", fn, reads, (), dur=1500, lat=lat, n=sum(len(eng_of[q]) for q in others))
+
+    def arrive(sem, qs, key, ready):
+        add("R", sem, None, (), [key], n=sum(len(split(q)[0][r]) for q in qs), ready=ready)
+
+    prev = {}
+
+    def const(eng, sem, fn, reads, key, dur):
+        prev[sem] = add(eng, sem, lambda: [fn()], reads, [key], dur=dur, extra=[prev[sem]] if sem in prev else [])
+
+    def iota(key, out, pattern, cm, n, **kw):
+        const("G", "gk", lambda: g.iota(out, pattern, 0, cm, **kw), [], key, 130 + 1.66 * n)
+
+    def ts(key, out, in0, rk, s1, op0, s2=None, op1=None, n=128):
+        a = (out, in0, s1, None, op0) if op1 is None else (out, in0, s1, s2, op0, op1)
+        const("V", "vk", lambda: V.tensor_scalar(*a), rk.split(), key, vd(n))
+
+    def tc(name, in0, rk, *a):
+        ts(name, cf[name] if name in cf else ci[name], (cf[in0] if in0 in cf else ci[in0]), in0 + " " + rk, *a, n=1)
+
+    def tt(key, out, a, b, rk, op):
+        const("V", "vk", lambda: V.tensor_tensor(out, a, b, op), rk.split(), key, vd(256))
+
+    def ms(key, ap, v, n):
+        const("V", "vk", lambda: V.memset(ap, v), [], key, vd(n, 0.5))
+
+    def diag(name, out, v, rk=""):
+        ts(name, out, kf["mrow"], "mrow pcf " + rk, cf["pcf"], OP.is_equal, v, OP.mult)
+    small = dict(allow_small_or_imprecise_dtypes=True)
+    iota("pc", ci["pc"], [[0, 1]], 1, 1)
+    iota("mrow", kf["mrow"], [[1, 128]], 0, 128, **small)
+    iota("sm", kf["sm"], [[1, 8], [0, 16]], 0, 128, **small)
+    iota("im", kf["im"], [[0, 8], [1, 16]], 0, 128, **small)
+    ms("cl", T.cl[:, :], -512.0, 128)
+    ms("cr", T.cr[:, 0:64], 0.0, 64)
+    ms("cr", T.cr[:, 64:128], 256.0, 64)
+    tc("pcf", "pc", "", 1.0, OP.mult)
+    tc("psi", "pc", "", 4, OP.arith_shift_right)
+    tc("ii", "pc", "", 15, OP.bitwise_and)
+    tc("odd", "pc", "", 1, OP.bitwise_and)
+    tc("ps", "psi", "", 1.0, OP.mult)
+    tc("pi", "ii", "", 1.0, OP.mult)
+    tc("b1", "odd", "", -2048.0, OP.mult, BIG + 2048.0 - 2047.5, OP.add)
+    tc("b2", "odd", "", -2048.0, OP.mult, BIG + 2048.0, OP.add)
+    diag("ineg", kb["ineg"], -1.0)
+    diag("i64h", kh["i64h"], 64.0)
+    ts("onesb", kh["onesb"], kf["sm"], "sm ps", cf["ps"], OP.is_equal)
+    ts("same", kf["same"], kf["sm"], "sm ps", cf["ps"], OP.is_equal)
+    ts("le", kf["le"], kf["im"], "im pi", cf["pi"], OP.is_ge)
+    tt("tri", kh["tri"], kf["same"], kf["le"], "same le", OP.mult)
+    xok = ["xo%d" % c for c in range(NC)]
+    add("V", "xo", lambda: [V.tensor_scalar(T.xo[:, :], T.un0[:, :], -2048.0, None, OP.add)], ["un0"], xok, dur=vd(256))
+    ms("mmx", T.mmx[:, :], 0.0, 1024)
+    ms("mmx", T.mmx[:, 0:1024:32], -512.0, 32)
+    ms("mmn", T.mmn[:, :], 0.0, 1024)
+    ms("mmn", T.mmn[:, 0:1024:32], 512.0, 32)
+
+    send(["su"], lambda q: T.su[big(q), :], T.lu[big(r), :], "au", 5000)
+    send(["st"], lambda q: T.st[big(q), :], T.lsh[big(r), :], "ash%d" % r, 9000)
+    iota("row8", T.row8[:, :], [[1, 8]], 0, 8, **small)
+    iota("negv", T.negv[0:1, :], [[0, 4], [-1, 128]], 0, 512, **small)
+    arrive("au", others, "lu", 10000.0)
+    add("Y", "dut", lambda: [g.sync.dma_start(T.uns[rows(q), :], T.units[rows(r), :] if q == r else T.lu[big(q), :]) for q in range(4)],
+        ["lu"], ["uns"], dur=400, lat=2000, n=4, inc=16)
+
+    def bounce(q):
+        arrive("ash%d" % q, [q], "lsh%d" % q, 12000.0 if q in near else 17000.0)
+        add("Y", "bs%d" % q, lambda: [g.sync.dma_start(T.shs[rows(q), :], T.lsh[big(q), :])], ["lsh%d" % q], ["shs%d" % q], dur=100, lat=3000, inc=16)
+    for q in near + off:
+        bounce(q)
+    slots = ["shs%d" % q for q in range(4)]
+
+    def measure(c, xb, xkey, shelf, skeys, b1, b2):
+        a, bk, b, o, v = T["pa%d" % c], ["pa%d" % c], T["pb%d" % c], 64 * c, 1024 * c
+        X, X0, X1, XY = a[:, 0:128], a[:, 0:64], a[:, 64:128], b[:, 384:448]
+        C = str(c)
+        w, wo = slice(o, o + 64), slice(o, o + 64, 2)
+        add("P", "pw" + C, lambda: [P.matmul(XY, kh["tri"], xb[:, w], True, False), P.matmul(b[:, 385:448:2], kh["onesb"], xb[:, wo], False, True)],
+            [xkey, "tri", "onesb"], (), ["pb" + C], dur=pe(2), n=2)
+        add("V", "y" + C, lambda: [V.tensor_scalar(T.y[:, w], XY, cf[b1], None, OP.add)], [b1], ["y" + C], ["pb" + C], dur=vd(64))
+        add("P", "px" + C, lambda: [P.matmul(X, T.cl[0:1, :], T.cr[0:1, :], True, False), P.matmul(X1, kh["i64h"], xb[:, w], False, False),
+                                    P.matmul(X0, kh["tri"], xb[:, w], False, False), P.matmul(a[:, 1:64:2], kh["onesb"], xb[:, wo], False, False)],
+            [xkey, "tri", "onesb", "cl", "cr", "i64h"], (), bk, dur=pe(5), n=4)
+        add("P", "py" + C, lambda: [P.matmul(X0, kb["ineg"], T.y[:, w], False, True)], ["y" + C, "ineg"], (), bk, dur=pe(1))
+        add("S", "sq" + C, lambda: [S.activation(T.sq[:, w], X0, AF.Square, bias=cf[b2])], [b2], ["sq" + C], bk, dur=sd(64))
+        add("V", "t" + C, lambda: [V.tensor_tensor(T.t3[:, w], T.sq[:, w], X1, OP.add)], ["sq" + C], ["t3" + C], bk, dur=vd(64))
+        add("V", "sf" + C, lambda: [V.tensor_scalar(T.sf[:, w], T.t3[:, w], 6, 4095, OP.arith_shift_right, OP.bitwise_and)], ["t3" + C], ["sf" + C],
+            dur=vd(64))
+        add("V", "of" + C, lambda: [V.tensor_copy(T.of[:, w], T.sf[:, w])], ["sf" + C], ["of" + C], dur=vd(64))
+        m = v + 32 * US
+        add("S", "ga" + C, lambda: [S.activation(T.ga[:, v:m], shelf[:, :].indirect(T.of[:, o:o + 2 * US]), AF.Copy)],
+            ["of" + C] + skeys, ["gas" + C], dur=sd(32 * US, GR))
+        gk = ["gas" + C]
+        if US < CU:
+            gk.append("gav" + C)
+            add("V", "gv" + C, lambda: [V.tensor_copy(T.ga[:, m:v + 1024], shelf[:, :].indirect(T.of[:, o + 2 * US:o + 64]))],
+                ["of" + C] + skeys, ["gav" + C], dur=50 + vd(32 * (CU - US), GR))
+        z = slice(v, v + 1024)
+        add("V", "mx" + C, lambda: [V.tensor_tensor_scan(T.mx[:, z], T.mmx[:, :], T.ga[:, z], 0.0, OP.add, OP.max)], gk + ["mmx"], ["mx" + C],
+            dur=vd(1024, 0.5))
+        add("V", "mn" + C, lambda: [V.tensor_tensor_scan(T.mn[:, z], T.mmn[:, :], T.ga[:, z], 0.0, OP.add, OP.min)], gk + ["mmn"], ["mn" + C],
+            dur=vd(1024, 0.5))
+
+    def ext(buf, c):
+        return buf[:, 1024 * c + 31:1024 * c + 1024:32]
+
+    def measure_all(shelf, skeys, b1, b2):
+        for c in range(NC):
+            measure(c, T.xo, "xo%d" % c, shelf, skeys, b1, b2)
+            add("V", "dd%d" % c, (lambda c: lambda: [V.tensor_tensor(T.dd[:, 32 * c:32 * c + 32], ext(T.mx, c), ext(T.mn, c), OP.subtract)])(c),
+                ["mx%d" % c, "mn%d" % c], ["dd%d" % c], dur=vd(64))
+    measure_all(T.sh0, ["sh0"], "b1", "b2")
+
+    ms("ones", kb["ones"], 1.0, 128)
+    ms("win", T.win[:, :], 0.0, 768)
+    for k, sh in ((0, 6), (1, 5)):
+        tc("bit%d" % k, "pc", "", sh, OP.arith_shift_right, 1, OP.bitwise_and)
+        tc("lam%d" % k, "bit%d" % k, "", -2.0, OP.mult, 1.0, OP.add)
+    ts("ind", T.ind[:, :], T.row8[:, :], "row8 ps", cf["ps"], OP.is_equal, 128.0, OP.mult, n=8)
+    ts("r1", T.r1[:, 0:2], T.ind[:, 2 * r:2 * r + 2], "ind", 1.0, OP.mult, n=2)
+    ts("r1", T.r1[:, 2:4], T.ind[:, 2 * r:2 * r + 2], "ind", -1.0, OP.mult, n=2)
+    for b in (0, 1):
+        ts("lp%d" % b, kb["lp%d" % b], kf["mrow"], "mrow ind", 0.0, OP.mult, T.ind[:, 2 * r + b:2 * r + b + 1], OP.add)
+        ts("ln%d" % b, kb["ln%d" % b], kb["lp%d" % b], "lp%d" % b, -1.0, OP.mult)
+    tc("va", "ps", "", float(2 * r), OP.is_ge)
+    tc("vb", "ps", "", float(2 * r + 1), OP.is_le)
+    tc("vv", "va", "vb", cf["vb"], OP.mult)
+    tc("vt", "ps", "", float(100 - 2 * r), OP.add)
+    tc("colr", "vt", "vv", cf["vv"], OP.mult, -100.0, OP.add)
+    for q in range(4):
+        ts("ql%d" % q, kb["ql%d" % q], kf["sm"], "sm colr", float(2 * q), OP.subtract, cf["colr"], OP.is_equal)
+    tc("fc", "ps", "", float(SFROM), OP.is_ge)
+    tc("scl2", "fc", "", -1.0, OP.mult, 2.0, OP.add)
+    tc("ad0", "fc", "", 127.0, OP.mult)
+    tc("ad1", "fc", "", 127.0, OP.mult, 1.0, OP.add)
+    tc("scl1", "fc", "", -0.5, OP.mult, 1.0, OP.add)
+    tc("ad2", "fc", "", 63.5, OP.mult, 256.0, OP.add)
+    diag("idf", kf["idf"], 1.0)
+
+    def round_consts(k):
+        K = str(k)
+        tc("px" + K, "lam" + K, "pcf", (64.0, 32.0)[k], OP.mult, cf["pcf"], OP.add)
+        tc("psx" + K, "lam" + K, "ps", (4.0, 2.0)[k], OP.mult, cf["ps"], OP.add)
+        tc("th" + K, "lam" + K, "", 0.5, OP.mult)
+        tc("nl" + K, "lam" + K, "", -1.0, OP.mult)
+        ts("pm" + K, kf["pm" + K], kf["mrow"], "mrow px" + K, cf["px" + K], OP.is_equal)
+        tt("dm" + K, kf["dm" + K], kf["pm" + K], kf["idf"], "idf pm" + K, OP.subtract)
+        ts("e1", kf["e1"], kf["sm"], "sm ps lam" + K, cf["ps"], OP.is_equal, cf["lam" + K], OP.mult)
+        ts("e2", kf["e2"], kf["sm"], "sm psx%s lam%s" % (K, K), cf["psx" + K], OP.is_equal, cf["lam" + K], OP.mult)
+        tt("sdp" + K, kb["sdp" + K], kf["e1"], kf["e2"], "e1 e2", OP.add)
+        ts("sdn" + K, kb["sdn" + K], kb["sdp" + K], "sdp" + K, -1.0, OP.mult)
+    round_consts(0)
+    diag("m16", kb["m16"], -16.0)
+    for t in range(1, 6):
+        h = HS[t] if t < 5 else 1
+        if t < 5:
+            tc("fi%d" % h, "pc", "", 16 - h, OP.bitwise_and)
+        tc("dc%d" % t, "fi%d" % h, "", -1.0, OP.mult, 16.0 - h if t < 5 else 15.5, OP.add)
+        diag("dg%d" % t, kb["dg%d" % t], cf["dc%d" % t], "dc%d" % t)
+        diag("idh%d" % HS[t - 1], kb["idh%d" % HS[t - 1]], float(HS[t - 1]))
+    diag("i64b", kb["i64b"], 64.0)
+
+    dkeys = ["dd%d" % c for c in range(NC)]
+    send(dkeys, lambda q: T.dd[:, :], T.dl[:, big(r)], "ad", 3000)
+    arrive("ad", others, "dl", 21000.0)
+    add("V", "srcu", lambda: [V.tensor_scalar(T.src[:, 128 * e:128 * e + 128], T.uns[:, e:256:2], -2048.0, None, OP.add) for e in (0, 1)],
+        ["uns"], ["srcA", "srcB"], dur=2 * vd(128), n=2)
+
+    def order(k):
+        pa2 = T.pa2
+        dq = [T.dd[:, :] if q == r or k else T.dl[:, big(q)] for q in range(4)]
+        dk = dkeys + ([] if k else ["dl"])
+        lks = ["lk%d" % s for s in range(8)] if k else ["lp0", "lp1", "ln0", "ln1"]
+
+        def lk(s):
+            return kb["lk%d" % s] if k else kb[("lp%d" if s < 4 else "ln%d") % (s % 2)]
+
+        def kcol():
+            o = [P.matmul(pa2[:, 0:8], T.negv[0:1, 0:128], ones8, True, False)]
+            if k:
+                return o + [P.matmul(pa2[:, 0:8], T.dd[:, :], T.r2[:, :], False, True)]
+            for q in range(4):
+                w = 0 if q < 2 else 2
+                o.append(P.matmul(pa2[:, 2 * q:2 * q + 2], dq[q], T.r1[:, w:w + 2], False, q == 3))
+            return o
+        add("P", "pkc", kcol, dk + ["negv", "ones", "r2" if k else "r1"], (), ["pa2"], dur=pe(3), n=2 if k else 5)
+        add("V", "kc", lambda: [V.tensor_copy(T.kc[:, :], pa2[:, 0:8])], (), ["kc"], ["pa2"], dur=vd(8))
+        places = [("pa0", list(range(0, 4))), ("pa1", list(range(SFROM, 8))), ("pa3", list(range(4, SFROM)))]
+
+        def krow(p, ss):
+            def fn():
+                o = [P.matmul(p[:, 0:128 * len(ss)], onesrow, T.negv[0:1, 0:128 * len(ss)], True, False)]
+                for j, s in enumerate(ss):
+                    o.append(P.matmul(p[:, big(j)], lk(s), dq[s // 2], False, j == len(ss) - 1))
+                return o
+            return fn
+
+        def compare(bn, j, s):
+            src, out = T[bn][:, big(j)], T.cc[:, :, 16 * s:16 * s + 16]
+            if bn == "pa1":
+                add("S", "cs", lambda: [S.activation(out, src, AF.Sign, bias=T.kc[:, s:s + 1], scale=-1.0)], ["kc"], ["cc%d" % s], [bn], dur=sd(128))
+            else:
+                add("V", "cv", lambda: [V.tensor_scalar(out, src, T.kc[:, s:s + 1], None, OP.is_lt)], ["kc"], ["cc%d" % s], [bn], dur=vd(128))
+        for bn, ss in places:
+            add("P", "pkr" + bn[2], krow(T[bn], ss), dk + lks + ["negv", "ones"], (), [bn], dur=pe(4 * len(ss)), n=1 + len(ss))
+        for bn, ss in places:
+            for j, s in enumerate(ss):
+                compare(bn, j, s)
+        qr = T.pb0[:, 0:128]
+        if k:
+            add("P", "pq", lambda: [P.matmul(qr, kb["sameb"], T.dd[:, :], True, True)], dk + ["sameb"], (), ["pb0"], dur=pe(2))
+        else:
+            add("P", "pq", lambda: [P.matmul(qr, kb["ql%d" % q], dq[q], q == 0, q == 3) for q in range(4)], dk + ["ql%d" % q for q in range(4)], (),
+                ["pb0"], dur=pe(8), n=4)
+        add("S", "sq_", lambda: [S.activation(T.src[:, 256:384], qr, AF.Copy)], (), ["srcq"], ["pb0"], dur=sd(128))
+        add("P", "pl", lambda: [P.matmul(pa2[:, 8 + j:9 + j], T.cc[:, j, :], ones1, True, True) for j in range(8)],
+            ["cc%d" % s for s in range(8)] + ["ones"], (), ["pa2"], dur=pe(8), n=8)
+        lists = [("scl2", "ad0"), ("scl2", "ad1"), ("scl1", "ad2")]
+        add("V", "po", lambda: [V.tensor_scalar(T.po[:, 8 * j:8 * j + 8], pa2[:, 8:16], cf[a], cf[b], OP.mult, OP.add) for j, (a, b) in enumerate(lists)],
+            ["scl2", "ad0", "ad1", "scl1", "ad2"], ["po"], ["pa2"], dur=3 * vd(8), n=3)
+        add("V", "scat", lambda: [V.tensor_copy(T.win[:, :].indirect(T.po[:, :]), T.src[:, :])], ["po", "srcA", "srcB", "srcq"], ["win"],
+            dur=50 + vd(384, 3.0))
+
+    def spap(c, t, st=1):
+        return T.sp[:, 320 * c + 64 * (t - 1):320 * c + 64 * t:st]
+
+    def pre_g(c, t):
+        C, w, b = str(c), slice(64 * c, 64 * c + 64), T["pb%d" % c]
+        G = b[:, 64:128]
+
+        def fn():
+            o = [P.matmul(G, kb["dg%d" % t], T.sg[:, w], True, False),
+                 P.matmul(b[:, 65:128:2], kb["m16"], T.sg[:, 64 * c + 1:64 * c + 64:2], False, False)]
+            for u in range(1, t):
+                o.append(P.matmul(G, kb["idh%d" % HS[u - 1]], spap(c, u), False, False))
+            if t == 5:
+                o.append(P.matmul(G, kb["i64b"], T.nt[:, w], False, False))
+            return o
+        n = t + 1 + (1 if t == 5 else 0)
+        add("P", "pg" + C, fn, ["sg" + C, "dg%d" % t, "m16"] + ["sp%d_%d" % (c, u) for u in range(1, t)] + ["idh%d" % HS[u - 1] for u in range(1, t)]
+            + (["i64b", "nt" + C] if t == 5 else []), (), ["pb" + C], dur=pe(n), n=n)
+
+    def start_chunk(k, c):
+        b, bk, o, W, C, K = T["pb%d" % c], ["pb%d" % c], 64 * c, T.win, str(c), str(k)
+        pm, dm, idf, dqp, w = kf["pm" + K], kf["dm" + K], kf["idf"], b[:, 320:384], slice(64 * c, 64 * c + 64)
+        add("P", "pD" + C, lambda: [P.matmul(b[:, 256:320:2], pm, W[:, o:o + 64:2], True, True),
+                                    P.matmul(b[:, 257:320:2], idf, W[:, o + 1:o + 64:2], True, True)], ["win", "pm" + K, "idf"], (), bk, dur=pe(8), n=2)
+        add("V", "x" + C, lambda: [V.tensor_copy(T.x[:, o:o + 64], b[:, 256:320])], (), ["x" + C], bk, dur=vd(64))
+        qw = slice(256 + 32 * c, 288 + 32 * c)
+        add("P", "pD" + C, lambda: [P.matmul(b[:, 128:192], dm, W[:, o:o + 64], True, True), P.matmul(b[:, 192:256], idf, W[:, o:o + 64], True, True),
+                                    P.matmul(b[:, 320:384:2], dm, W[:, qw], True, True), P.matmul(b[:, 321:384:2], dm, W[:, qw], True, True)],
+            ["win", "dm" + K, "idf"], (), bk, dur=pe(16), n=4)
+        add("S", "sg" + C, lambda: [S.activation(T.sg[:, w], dqp, AF.Sign, bias=-0.5, scale=cf["nl" + K])], ["nl" + K], ["sg" + C], bk, dur=sd(64))
+        add("V", "nt" + C, lambda: [V.tensor_scalar(T.nt[:, w], dqp, cf["th" + K], None, OP.is_le)], ["th" + K], ["nt" + C], bk, dur=vd(64))
+
+    def trial(k, c, t, b1, b2):
+        b, bk, a, o, C, K = T["pb%d" % c], ["pb%d" % c], T["pa%d" % c], 64 * c, str(c), str(k)
+        w, w3, sp, h = slice(o, o + 64), slice(32 * c, 32 * c + 32), "sp%d_%d" % (c, t), "idh%d" % HS[t - 1]
+        measure(c, T.x, "x" + C, T.shs, slots, b1, b2)
+        pre_g(c, t)
+        add("P", "pd" + C, lambda: [P.matmul(a[:, 128 + e:192:2], kb[n + K], ext(m, c), n == "sdp", n == "sdn")
+                                    for e in (0, 1) for n, m in (("sdp", T.mx), ("sdn", T.mn))],
+            ["mx" + C, "mn" + C, "sdp" + K, "sdn" + K], (), ["pa" + C], dur=pe(4), n=4)
+        add("V", "sp" + C, lambda: [V.tensor_scalar(spap(c, t), a[:, 128:192], 0.0, -0.5, OP.is_gt, OP.add)], (), [sp], ["pa" + C], dur=vd(64))
+        add("P", "pc" + C, lambda: [P.matmul(b[:, 64:128], kb[h], spap(c, t), False, True)], [sp, h], (), bk, dur=pe(1))
+        add("V", "mk" + C, lambda: [V.tensor_scalar(T.mk[:, w], b[:, 64:128], 0.0, None, OP.is_equal)], (), ["mk" + C], bk, dur=vd(64))
+        add("V", "md" + C, lambda: [V.tensor_tensor(T.md[:, w], T.mk[:, w], b[:, 128:192], OP.mult)], ["mk" + C], ["md" + C], bk, dur=vd(64))
+        nm, dst = ("x", T.x) if t < 5 else ("nw", T.nw)
+        add("V", nm + C, lambda: [V.tensor_tensor(dst[:, w], T.md[:, w], b[:, 192:256], OP.add)], ["md" + C], [nm + C], bk, dur=vd(64))
+        if t == 5 and k == 0:
+            add("P", "fs" + C, lambda: [P.matmul(b[:, 448:480], kb["idh%d" % HS[u - 1]], spap(c, u, 2), u == 1, u == 5) for u in range(1, 6)],
+                ["sp%d_%d" % (c, u) for u in range(1, 6)], (), bk, dur=pe(5), n=5)
+            add("V", "pf" + C, lambda: [V.tensor_tensor(T.pf[:, w3], T.sg[:, o:o + 64:2], b[:, 448:480], OP.mult)], ["sg" + C], ["pf" + C], bk, dur=vd(32))
+
+    def trials(k, b1, b2):
+        for c in range(NC):
+            start_chunk(k, c)
+        for t in range(1, 6):
+            for c in range(NC):
+                trial(k, c, t, b1, b2)
+    order(0)
+    trials(0, "b1", "b2")
+    ts("r2t", T.r2t[:, :], T.row8[:, :], "row8 ps lam1", cf["ps"], OP.is_equal, cf["lam1"], OP.mult, n=8)
+    ts("r2f", T.r2f[:, :], T.r2t[:, :], "r2t", 128.0, OP.mult, n=8)
+    ts("r2", T.r2[:, :], T.r2t[:, :], "r2t", 128.0, OP.mult, n=8)
+    for s in range(8):
+        ts("lk%d" % s, kb["lk%d" % s], kf["mrow"], "mrow r2f", 0.0, OP.mult, T.r2f[:, s:s + 1], OP.add)
+    ts("sameb", kb["sameb"], kf["sm"], "sm ps", cf["ps"], OP.is_equal)
+    round_consts(1)
+    nwk = ["nw%d" % c for c in range(NC)] + ["po"]
+    add("S", "un1", lambda: [S.activation(T.src[:, 0:128], T.nw[:, :].indirect(T.po[:, 0:8]), AF.Copy)], nwk, ["srcA"], dur=sd(128, GR))
+    add("V", "un2", lambda: [V.tensor_copy(T.src[:, 128:256], T.nw[:, :].indirect(T.po[:, 8:16]))], nwk, ["srcB"], dur=50 + vd(128, GR))
+    add("V", "xo", lambda: [V.tensor_copy(T.xo[:, e:256:2], T.src[:, 128 * e:128 * e + 128]) for e in (0, 1)], ["srcA", "srcB"], xok, dur=2 * vd(128), n=2)
+    add("V", "red", lambda: [V.tensor_reduce(cf["asum"], T.pf[:, :], AxisListType.X, OP.add)], ["pf%d" % c for c in range(NC)], ["asum"], dur=vd(128))
+    add("V", "red", lambda: [V.tensor_scalar(cf["nb" + e], cf["asum"], cf["b" + e], 1984.0, OP.add, OP.add) for e in "12"], ["asum", "b1", "b2"],
+        ["nb1", "nb2"], dur=2 * vd(1), n=2)
+    measure_all(T.shs, slots, "nb1", "nb2")
+    order(1)
+    send(["srcq"], lambda q: T.src[:, 256:384], T.lq[:, big(r)], "aq", 3000)
+    arrive("aq", others, "lq", 90000.0)
+
+    def yq():
+        o = []
+        for b in (0, 1):
+            p = 32 * r + 16 * b
+            for q in range(4):
+                s = T.src[p:p + 1, 256:384] if q == r else T.lq[p:p + 1, big(q)]
+                o.append(g.sync.dma_start(T.yq[2 * q + b:2 * q + b + 1, :], s))
+        return o
+    add("Y", "douq", yq, ["srcq", "lq"], ["yq"], dur=800, lat=2000, n=8, inc=16)
+    trials(1, "nb1", "nb2")
+
+    add("S", "un1", lambda: [S.activation(T.ou[:, 0:256:2], T.nw[:, :].indirect(T.po[:, 0:8]), AF.Identity, bias=2048.0)], nwk, ["ouA"], dur=sd(128, GR))
+    add("V", "un2", lambda: [V.tensor_scalar(T.ou[:, 1:256:2], T.nw[:, :].indirect(T.po[:, 8:16]), 2048.0, None, OP.add)], nwk, ["ouB"],
+        dur=50 + vd(128, GR))
+
+    def copies(eng, sem, cps, reads, key):
+        def fn():
+            return [V.tensor_copy(d, s) if eng == "V" else S.activation(d, s, AF.Copy) for d, s in cps]
+        add(eng, sem, fn, reads, [key], dur=(vd(64) if eng == "V" else sd(64)) * len(cps), n=len(cps))
+    blocks = [(T.sto[32 * a:32 * a + 32, 64 * q:64 * q + 64], T.ou[rows(q), 64 * a:64 * a + 64]) for q in others for a in range(4)]
+    copies("V", "x0", blocks[:7], ["ouA", "ouB"], "stoV")
+    copies("S", "sq0", blocks[7:], ["ouA", "ouB"], "stoS")
+    send(["stoV", "stoS"], lambda q: T.sto[:, 64 * q:64 * q + 64], T.lr[:, 64 * r:64 * r + 64], "al%d" % r, 3000)
+    add("Y", "dou", lambda: [g.sync.dma_start(T.yu[rows(r), :], T.ou[rows(r), :])], ["ouA", "ouB"], ["yu"], dur=100, lat=2000, inc=16)
+
+    def back(j, q):
+        arrive("al%d" % q, [q], "lr%d" % q, 1e6 + 1000.0 * j)
+        cps = [(T.yo[rows(q), 64 * a:64 * a + 64], T.lr[32 * a:32 * a + 32, 64 * q:64 * q + 64]) for a in range(4)]
+        m = 3 if j < 2 else 2
+        copies("V", "x1", cps[:m], ["lr%d" % q], "yoV%d" % q)
+        copies("S", "sq1", cps[m:], ["lr%d" % q], "yoS%d" % q)
+        add("Y", "dou", lambda: [g.sync.dma_start(T.yu[rows(q), :], T.yo[rows(q), :])], ["yoV%d" % q, "yoS%d" % q], ["yu%d" % q], dur=100, lat=2000, inc=16)
+    for j, q in enumerate(near + off):
+        back(j, q)
+    return emit(T, dict(V=V, S=S, P=P, G=g, Y=g.sync), tasks, count)
+
+
+def stage(t):
+    return t["sem"].rstrip("0123456789")
+
+
+def emit(T, E, tasks, count):
+    n = len(tasks)
+    succ, soft, before = [[] for _ in range(n)], [[] for _ in range(n)], {}
+    for i, t in enumerate(tasks):
+        if t["sem"] in before and tasks[before[t["sem"]]]["eng"] == t["eng"]:
+            t["soft"].add(before[t["sem"]])
+        before[t["sem"]] = i
+        for d in t["deps"]:
+            succ[d].append(i)
+        for d in t["soft"] - t["deps"]:
+            soft[d].append(i)
+    need = [len(t["deps"] | t["soft"]) for t in tasks]
+    rest, prio = [0.0] * n, [0.0] * n
+    for i in range(n - 1, -1, -1):
+        t = tasks[i]
+        rest[i] = t["dur"] + t["lat"] + max([rest[j] + WAKE for j in succ[i]] or [0.0])
+        b = stage(t)
+        prio[i] = rest[i] + BIAS.get(b, 0.0) + (LANEB * (3 - int(t["sem"][len(b):])) if b != t["sem"] and len(b) <= 2 else 0.0)
+    look = [SCLA if stage(t) in ("mx", "mn") else GALA if stage(t) == "ga" else 0.0 for t in tasks]
+    est, fin, free, seq = [t["ready"] for t in tasks], [0.0] * n, {}, {}
+    pool = set(i for i in range(n) if need[i] == 0)
+    while pool:
+        best = None
+        for i in pool:
+            s = max(est[i], free.get(tasks[i]["eng"], 0.0))
+            key = (round((s + look[i]) / BUCKET), -prio[i], i)
+            if best is None or key < best[0]:
+                best = (key, i, s)
+        _, i, s = best
+        pool.discard(i)
+        t = tasks[i]
+        if t["eng"] != "R":
+            free[t["eng"]] = s + t["dur"]
+        seq.setdefault(t["eng"], []).append(i)
+        fin[i] = s + t["dur"] + t["lat"]
+        for j in succ[i]:
+            est[j] = max(est[j], fin[i] + WAKE)
+        for j in succ[i] + soft[i]:
+            need[j] -= 1
+            if need[j] == 0:
+                pool.add(j)
+    clocks, after = {e: {} for e in E}, [None] * n
+    pos, left = {e: 0 for e in seq}, n
+    while left:
+        was = left
+        for e in seq:
+            while pos[e] < len(seq[e]):
+                i = seq[e][pos[e]]
+                t = tasks[i]
+                if any(after[d] is None for d in t["deps"]):
+                    break
+                ck = clocks.get(e, {})
+                if e != "R":
+                    for d in sorted(t["deps"], key=lambda d: -fin[d]):
+                        sem, val = tasks[d]["sem"], tasks[d]["val"]
+                        if ck.get(sem, 0) < val:
+                            E[e].wait_ge(T.sem[sem], int(val))
+                            for s, v in after[d].items():
+                                ck[s] = max(ck.get(s, 0), v)
+                    for ins in t["fn"]():
+                        ins.then_inc(T.sem[t["sem"]], t["inc"])
+                after[i] = dict(ck)
+                after[i][t["sem"]] = max(ck.get(t["sem"], 0), t["val"])
+                pos[e] += 1
+                left -= 1
+        assert left < was
+    for s in sorted(count):
+        E["P"].wait_ge(T.sem[s], int(count[s]))
+    return seq, fin, tasks

@@ -2,19 +2,18 @@ from concourse.bass import DstId, RemoteDMATransfer
 from concourse.mybir import dt, AluOpType as OP, AxisListType, ActivationFunctionType as AF
 
 NC, CU = 4, 32
-US = 28
+US, USM = 32, 24
 BIG = 786432.0
 HS = (16, 8, 4, 2, 1)
 SFROM = 5
-GR, VF, SFX, PEC, WAKE = 1.56, 12.0, 65.0, 0.71, 90.0
-BUCKET, LANEB, GALA, SCLA = 100.0, 1000.0, 400.0, 0.0
-BIAS = {"y": 1000.0, "sq": 1000.0, "t": 1000.0, "sf": 1000.0, "of": 1000.0, "x": 1000.0, "mk": 1000.0, "md": 1000.0, "sp": 1000.0,
-        "mn": 500.0, "vk": -2000.0, "ga": 1000.0}
+GR, VF, SFX, PEC, WAKE, ITERS = 1.56, 12.0, 65.0, 0.71, 110.0, 1
+LB = 1200.0
+SB = {"ga": -800.0, "mx": -800.0, "mn": -800.0, "mk": -800.0, "md": -800.0, "x": -800.0, "t": 800.0, "of": -800.0}
 
-F32M = ["mrow", "sm", "im", "idf", "le", "same", "pm0", "pm1", "dm0", "dm1", "e1", "e2"]
+F32M = ["mrow", "sm", "im", "idf", "le", "same", "pmt", "e1", "e2"]
 B16M = (["ineg", "i64b", "m16", "sameb", "ones", "sdp0", "sdn0", "sdp1", "sdn1", "lp0", "lp1", "ln0", "ln1"] + ["idh%d" % h for h in HS]
         + ["dg%d" % t for t in range(1, 6)] + ["lk%d" % s for s in range(8)] + ["ql%d" % q for q in range(4)])
-H16M = ["tri", "onesb", "i64h"]
+H16M = ["tri", "onesb", "i64h", "idd", "pm0", "pm1", "dm0", "dm1"]
 COLF = ["pcf", "ps", "pi", "b1", "b2", "nb1", "nb2", "asum", "lam0", "lam1", "px0", "px1", "psx0", "psx1", "th0", "th1", "nl0", "nl1",
         "va", "vb", "vv", "vt", "colr", "fc", "scl2", "ad0", "ad1", "scl1", "ad2"] + ["dc%d" % t for t in range(1, 6)]
 COLI = ["pc", "psi", "ii", "odd", "bit0", "bit1"] + ["fi%d" % h for h in (8, 4, 2, 1)]
@@ -22,11 +21,11 @@ SCRATCH = {"cc": ("sbuf", [128, 8, 128], "bfloat16"), "st": ("dram", [512, 1024]
            "lsh": ("dram", [512, 1024], "bfloat16"), "lu": ("dram", [512, 64], "int32")}
 for _d, _l in (("float32", (("kf", 128 * len(F32M)), ("cf", len(COLF)), ("row8", 8), ("ind", 8), ("r2t", 8), ("r2f", 8), ("sq", 256), ("md", 256),
                             ("pf", 128), ("nw", 256), ("kc", 8), ("src", 384), ("win", 384), ("ou", 256), ("sto", 256), ("lr", 256), ("yo", 256),
-                            ("lq", 512))),
+                            ("qo", 128), ("lq", 512))),
                ("bfloat16", (("kb", 128 * len(B16M)), ("r1", 4), ("r2", 8), ("negv", 512), ("cl", 128), ("cr", 128), ("mmx", 1024), ("mmn", 1024),
                              ("sh0", 4096), ("shs", 4096), ("y", 256), ("ga", 4096), ("mx", 4096), ("mn", 4096), ("mk", 256), ("sp", 1280),
                              ("sg", 256), ("nt", 256), ("dd", 128), ("dl", 512))),
-               ("float16", (("kh", 128 * len(H16M)), ("xo", 256), ("x", 256))),
+               ("float16", (("kh", 128 * len(H16M)), ("xo", 256), ("x", 256), ("wh", 384))),
                ("int32", (("ci", len(COLI)), ("un0", 256), ("uns", 256), ("t3", 256), ("sf", 256))),
                ("uint16", (("of", 256), ("po", 24)))):
     for _n, _w in _l:
@@ -34,8 +33,9 @@ for _d, _l in (("float32", (("kf", 128 * len(F32M)), ("cf", len(COLF)), ("row8",
 for _i in range(4):
     SCRATCH["pa%d" % _i] = ("psum", [128, 512], "float32")
     SCRATCH["pb%d" % _i] = ("psum", [128, 512], "float32")
-LANE = "pw px y py sq t sf of ga gv mx mn pd sp pg pc mk md x pD sg nt nw fs pf dd".split()
-ONE = "vk gk srcu xo pkc kc pkr0 pkr1 pkr3 cv cs pq sq_ pl po scat red un1 un2 dst dsu dun dsh dut douq dou au ad aq loc".split()
+LANE = "pw px y py sq t sf of ga gv mx mn pd sp pg pc mk md x pD sg nt nw pf dd".split()
+ONE = ("vk gk srcu xo pkc kc pk0 pk1 pk3 pkr0 pkr1 pkr3 cv cs pq sq_ pl po poq scat scq whq red un1 un2 dst dsu dun dsh dut douq dou "
+       "au ad aq loc").split()
 SEMAPHORES = [s + str(c) for s in LANE for c in range(NC)] + ONE + [s + str(q) for s in ("ash", "bs", "al") for q in range(4)]
 
 
@@ -60,7 +60,7 @@ def rank_program(g, core, T, topo):
     V, S, P = g.vector, g.scalar, g.tensor
     tasks, lastw, readers, bank, count = [], {}, {}, {}, {}
 
-    def add(eng, sem, fn, reads=(), writes=(), banks=(), dur=60.0, lat=0.0, n=1, inc=1, ready=0.0, extra=()):
+    def add(eng, sem, fn, reads=(), writes=(), banks=(), dur=60.0, lat=0.0, n=1, inc=1, extra=()):
         i = len(tasks)
         deps, soft = set(extra), set()
         for k in list(reads) + list(writes):
@@ -81,7 +81,7 @@ def rank_program(g, core, T, topo):
             lastw[k] = i
             readers[k] = []
         count[sem] = count.get(sem, 0) + n * inc
-        tasks.append(dict(eng=eng, sem=sem, val=count[sem], inc=inc, fn=fn, deps=deps, soft=soft - deps, dur=dur, lat=lat, ready=ready))
+        tasks.append(dict(eng=eng, sem=sem, val=count[sem], inc=inc, fn=fn, deps=deps, soft=soft - deps, dur=dur, lat=lat))
         return i
 
     def mats(buf, names):
@@ -100,8 +100,8 @@ def rank_program(g, core, T, topo):
     add("S", "dun", lambda: [S.dma_start(T.un0[:, :], T.units[:, :])], (), ["un0"], dur=100, lat=2000, inc=16)
     add("Y", "dst", lambda: [g.sync.dma_start(T.st[big(q), :], T.shelf[rows(q), :]) for q in others], (), ["st"], dur=300, lat=4000, n=3, inc=16)
     add("S", "dsu", lambda: [S.dma_start(T.su[big(q), :], T.units[rows(q), :]) for q in others], (), ["su"], dur=300, lat=2000, n=3, inc=16)
-    add("Y", "dsh", lambda: [g.sync.dma_start(T.sh0[:, :], T.shelf[:, :])], (), ["sh0"], dur=100, lat=6000, inc=16)
-    add("Y", "bs%d" % r, lambda: [g.sync.dma_start(T.shs[rows(r), :], T.shelf[rows(r), :])], (), ["shs%d" % r], dur=100, lat=7000, inc=16)
+    add("Y", "dsh", lambda: [g.sync.dma_start(T.sh0[:, :], T.shelf[:, :])], (), ["sh0"], dur=100, lat=7000, inc=16)
+    add("Y", "bs%d" % r, lambda: [g.sync.dma_start(T.shs[rows(r), :], T.shelf[rows(r), :])], (), ["shs%d" % r], dur=100, lat=8000, inc=16)
 
     def split(p):
         oth = [q for q in range(4) if q != p]
@@ -116,7 +116,7 @@ def rank_program(g, core, T, topo):
     eng_of, off = split(r)
     near = [q for q in others if q not in off]
 
-    def send(reads, src_of, dst, sem, lat):
+    def send(reads, src_of, dst, sem):
         def fn():
             tr = []
             for q in others:
@@ -125,10 +125,10 @@ def rank_program(g, core, T, topo):
                                             remote_sem=T.sem[sem], src=src_of(q), dst=dst))
             g.remote_dma_fused(tr, local_sem=T.sem["loc"])
             return []
-        add("G", "loc", fn, reads, (), dur=1500, lat=lat, n=sum(len(eng_of[q]) for q in others))
+        return add("G", "loc", fn, reads, (), dur=1500, n=sum(len(eng_of[q]) for q in others))
 
-    def arrive(sem, qs, key, ready):
-        add("R", sem, None, (), [key], n=sum(len(split(q)[0][r]) for q in qs), ready=ready)
+    def arrive(sem, qs, key, like, lat):
+        add("R", sem, None, (), [key], dur=0.0, lat=lat, n=sum(len(split(q)[0][r]) for q in qs), extra=[like])
 
     prev = {}
 
@@ -169,35 +169,35 @@ def rank_program(g, core, T, topo):
     tc("pi", "ii", "", 1.0, OP.mult)
     tc("b1", "odd", "", -2048.0, OP.mult, BIG + 2048.0 - 2047.5, OP.add)
     tc("b2", "odd", "", -2048.0, OP.mult, BIG + 2048.0, OP.add)
-    diag("ineg", kb["ineg"], -1.0)
-    diag("i64h", kh["i64h"], 64.0)
-    ts("onesb", kh["onesb"], kf["sm"], "sm ps", cf["ps"], OP.is_equal)
     ts("same", kf["same"], kf["sm"], "sm ps", cf["ps"], OP.is_equal)
     ts("le", kf["le"], kf["im"], "im pi", cf["pi"], OP.is_ge)
     tt("tri", kh["tri"], kf["same"], kf["le"], "same le", OP.mult)
+    ts("onesb", kh["onesb"], kf["sm"], "sm ps", cf["ps"], OP.is_equal)
     xok = ["xo%d" % c for c in range(NC)]
     add("V", "xo", lambda: [V.tensor_scalar(T.xo[:, :], T.un0[:, :], -2048.0, None, OP.add)], ["un0"], xok, dur=vd(256))
+    diag("ineg", kb["ineg"], -1.0)
+    diag("i64h", kh["i64h"], 64.0)
     ms("mmx", T.mmx[:, :], 0.0, 1024)
     ms("mmx", T.mmx[:, 0:1024:32], -512.0, 32)
     ms("mmn", T.mmn[:, :], 0.0, 1024)
     ms("mmn", T.mmn[:, 0:1024:32], 512.0, 32)
 
-    send(["su"], lambda q: T.su[big(q), :], T.lu[big(r), :], "au", 5000)
-    send(["st"], lambda q: T.st[big(q), :], T.lsh[big(r), :], "ash%d" % r, 9000)
+    s_u = send(["su"], lambda q: T.su[big(q), :], T.lu[big(r), :], "au")
+    s_s = send(["st"], lambda q: T.st[big(q), :], T.lsh[big(r), :], "ash%d" % r)
     iota("row8", T.row8[:, :], [[1, 8]], 0, 8, **small)
     iota("negv", T.negv[0:1, :], [[0, 4], [-1, 128]], 0, 512, **small)
-    arrive("au", others, "lu", 10000.0)
+    arrive("au", others, "lu", s_u, 3500.0)
     add("Y", "dut", lambda: [g.sync.dma_start(T.uns[rows(q), :], T.units[rows(r), :] if q == r else T.lu[big(q), :]) for q in range(4)],
         ["lu"], ["uns"], dur=400, lat=2000, n=4, inc=16)
 
     def bounce(q):
-        arrive("ash%d" % q, [q], "lsh%d" % q, 12000.0 if q in near else 17000.0)
+        arrive("ash%d" % q, [q], "lsh%d" % q, s_s, 6000.0 if q in near else 10000.0)
         add("Y", "bs%d" % q, lambda: [g.sync.dma_start(T.shs[rows(q), :], T.lsh[big(q), :])], ["lsh%d" % q], ["shs%d" % q], dur=100, lat=3000, inc=16)
     for q in near + off:
         bounce(q)
     slots = ["shs%d" % q for q in range(4)]
 
-    def measure(c, xb, xkey, shelf, skeys, b1, b2):
+    def measure(c, xb, xkey, shelf, skeys, b1, b2, us):
         a, bk, b, o, v = T["pa%d" % c], ["pa%d" % c], T["pb%d" % c], 64 * c, 1024 * c
         X, X0, X1, XY = a[:, 0:128], a[:, 0:64], a[:, 64:128], b[:, 384:448]
         C = str(c)
@@ -214,18 +214,19 @@ def rank_program(g, core, T, topo):
         add("V", "sf" + C, lambda: [V.tensor_scalar(T.sf[:, w], T.t3[:, w], 6, 4095, OP.arith_shift_right, OP.bitwise_and)], ["t3" + C], ["sf" + C],
             dur=vd(64))
         add("V", "of" + C, lambda: [V.tensor_copy(T.of[:, w], T.sf[:, w])], ["sf" + C], ["of" + C], dur=vd(64))
-        m = v + 32 * US
-        add("S", "ga" + C, lambda: [S.activation(T.ga[:, v:m], shelf[:, :].indirect(T.of[:, o:o + 2 * US]), AF.Copy)],
-            ["of" + C] + skeys, ["gas" + C], dur=sd(32 * US, GR))
+        m = v + 32 * us
+        add("S", "ga" + C, lambda: [S.activation(T.ga[:, v:m], shelf[:, :].indirect(T.of[:, o:o + 2 * us]), AF.Copy)],
+            ["of" + C] + skeys, ["gas" + C], dur=sd(32 * us, GR))
         gk = ["gas" + C]
-        if US < CU:
+        if us < CU:
             gk.append("gav" + C)
-            add("V", "gv" + C, lambda: [V.tensor_copy(T.ga[:, m:v + 1024], shelf[:, :].indirect(T.of[:, o + 2 * US:o + 64]))],
-                ["of" + C] + skeys, ["gav" + C], dur=50 + vd(32 * (CU - US), GR))
+            add("V", "gv" + C, lambda: [V.tensor_copy(T.ga[:, m:v + 1024], shelf[:, :].indirect(T.of[:, o + 2 * us:o + 64]))],
+                ["of" + C] + skeys, ["gav" + C], dur=50 + vd(32 * (CU - us), GR))
         z = slice(v, v + 1024)
-        add("V", "mx" + C, lambda: [V.tensor_tensor_scan(T.mx[:, z], T.mmx[:, :], T.ga[:, z], 0.0, OP.add, OP.max)], gk + ["mmx"], ["mx" + C],
+        gr = ["gas" + C, "gav" + C]
+        add("V", "mx" + C, lambda: [V.tensor_tensor_scan(T.mx[:, z], T.mmx[:, :], T.ga[:, z], 0.0, OP.add, OP.max)], gr + ["mmx"], ["mx" + C],
             dur=vd(1024, 0.5))
-        add("V", "mn" + C, lambda: [V.tensor_tensor_scan(T.mn[:, z], T.mmn[:, :], T.ga[:, z], 0.0, OP.add, OP.min)], gk + ["mmn"], ["mn" + C],
+        add("V", "mn" + C, lambda: [V.tensor_tensor_scan(T.mn[:, z], T.mmn[:, :], T.ga[:, z], 0.0, OP.add, OP.min)], gr + ["mmn"], ["mn" + C],
             dur=vd(1024, 0.5))
 
     def ext(buf, c):
@@ -233,16 +234,12 @@ def rank_program(g, core, T, topo):
 
     def measure_all(shelf, skeys, b1, b2):
         for c in range(NC):
-            measure(c, T.xo, "xo%d" % c, shelf, skeys, b1, b2)
+            measure(c, T.xo, "xo%d" % c, shelf, skeys, b1, b2, USM)
             add("V", "dd%d" % c, (lambda c: lambda: [V.tensor_tensor(T.dd[:, 32 * c:32 * c + 32], ext(T.mx, c), ext(T.mn, c), OP.subtract)])(c),
                 ["mx%d" % c, "mn%d" % c], ["dd%d" % c], dur=vd(64))
     measure_all(T.sh0, ["sh0"], "b1", "b2")
 
     ms("ones", kb["ones"], 1.0, 128)
-    ms("win", T.win[:, :], 0.0, 768)
-    for k, sh in ((0, 6), (1, 5)):
-        tc("bit%d" % k, "pc", "", sh, OP.arith_shift_right, 1, OP.bitwise_and)
-        tc("lam%d" % k, "bit%d" % k, "", -2.0, OP.mult, 1.0, OP.add)
     ts("ind", T.ind[:, :], T.row8[:, :], "row8 ps", cf["ps"], OP.is_equal, 128.0, OP.mult, n=8)
     ts("r1", T.r1[:, 0:2], T.ind[:, 2 * r:2 * r + 2], "ind", 1.0, OP.mult, n=2)
     ts("r1", T.r1[:, 2:4], T.ind[:, 2 * r:2 * r + 2], "ind", -1.0, OP.mult, n=2)
@@ -261,17 +258,24 @@ def rank_program(g, core, T, topo):
     tc("ad0", "fc", "", 127.0, OP.mult)
     tc("ad1", "fc", "", 127.0, OP.mult, 1.0, OP.add)
     tc("scl1", "fc", "", -0.5, OP.mult, 1.0, OP.add)
-    tc("ad2", "fc", "", 63.5, OP.mult, 256.0, OP.add)
+    tc("ad2", "fc", "", 63.5, OP.mult)
+    ms("win", T.win[:, 0:256], 0.0, 512)
+    ms("winq", T.win[:, 256:384], 0.0, 256)
+    for k, sh in ((0, 6), (1, 5)):
+        tc("bit%d" % k, "pc", "", sh, OP.arith_shift_right, 1, OP.bitwise_and)
+        tc("lam%d" % k, "bit%d" % k, "", -2.0, OP.mult, 1.0, OP.add)
     diag("idf", kf["idf"], 1.0)
+    diag("idd", kh["idd"], 1.0)
 
     def round_consts(k):
         K = str(k)
         tc("px" + K, "lam" + K, "pcf", (64.0, 32.0)[k], OP.mult, cf["pcf"], OP.add)
-        tc("psx" + K, "lam" + K, "ps", (4.0, 2.0)[k], OP.mult, cf["ps"], OP.add)
-        tc("th" + K, "lam" + K, "", 0.5, OP.mult)
+        ts("pm" + K, kh["pm" + K], kf["mrow"], "mrow px" + K, cf["px" + K], OP.is_equal)
+        ts("pmt", kf["pmt"], kf["mrow"], "mrow px" + K, cf["px" + K], OP.is_equal)
+        tt("dm" + K, kh["dm" + K], kf["pmt"], kf["idf"], "idf pmt", OP.subtract)
         tc("nl" + K, "lam" + K, "", -1.0, OP.mult)
-        ts("pm" + K, kf["pm" + K], kf["mrow"], "mrow px" + K, cf["px" + K], OP.is_equal)
-        tt("dm" + K, kf["dm" + K], kf["pm" + K], kf["idf"], "idf pm" + K, OP.subtract)
+        tc("th" + K, "lam" + K, "", 0.5, OP.mult)
+        tc("psx" + K, "lam" + K, "ps", (4.0, 2.0)[k], OP.mult, cf["ps"], OP.add)
         ts("e1", kf["e1"], kf["sm"], "sm ps lam" + K, cf["ps"], OP.is_equal, cf["lam" + K], OP.mult)
         ts("e2", kf["e2"], kf["sm"], "sm psx%s lam%s" % (K, K), cf["psx" + K], OP.is_equal, cf["lam" + K], OP.mult)
         tt("sdp" + K, kb["sdp" + K], kf["e1"], kf["e2"], "e1 e2", OP.add)
@@ -288,8 +292,8 @@ def rank_program(g, core, T, topo):
     diag("i64b", kb["i64b"], 64.0)
 
     dkeys = ["dd%d" % c for c in range(NC)]
-    send(dkeys, lambda q: T.dd[:, :], T.dl[:, big(r)], "ad", 3000)
-    arrive("ad", others, "dl", 21000.0)
+    s_d = send(dkeys, lambda q: T.dd[:, :], T.dl[:, big(r)], "ad")
+    arrive("ad", others, "dl", s_d, 3500.0)
     add("V", "srcu", lambda: [V.tensor_scalar(T.src[:, 128 * e:128 * e + 128], T.uns[:, e:256:2], -2048.0, None, OP.add) for e in (0, 1)],
         ["uns"], ["srcA", "srcB"], dur=2 * vd(128), n=2)
 
@@ -310,17 +314,15 @@ def rank_program(g, core, T, topo):
                 w = 0 if q < 2 else 2
                 o.append(P.matmul(pa2[:, 2 * q:2 * q + 2], dq[q], T.r1[:, w:w + 2], False, q == 3))
             return o
-        add("P", "pkc", kcol, dk + ["negv", "ones", "r2" if k else "r1"], (), ["pa2"], dur=pe(3), n=2 if k else 5)
-        add("V", "kc", lambda: [V.tensor_copy(T.kc[:, :], pa2[:, 0:8])], (), ["kc"], ["pa2"], dur=vd(8))
         places = [("pa0", list(range(0, 4))), ("pa1", list(range(SFROM, 8))), ("pa3", list(range(4, SFROM)))]
 
-        def krow(p, ss):
-            def fn():
-                o = [P.matmul(p[:, 0:128 * len(ss)], onesrow, T.negv[0:1, 0:128 * len(ss)], True, False)]
-                for j, s in enumerate(ss):
-                    o.append(P.matmul(p[:, big(j)], lk(s), dq[s // 2], False, j == len(ss) - 1))
-                return o
-            return fn
+        def kconst(bn, n):
+            add("P", "pk" + bn[2], lambda: [P.matmul(T[bn][:, 0:128 * n], onesrow, T.negv[0:1, 0:128 * n], True, False)], ["negv", "ones"], (), [bn],
+                dur=pe(2 * n))
+
+        def krow(bn, ss):
+            add("P", "pkr" + bn[2], lambda: [P.matmul(T[bn][:, big(j)], lk(s), dq[s // 2], False, j == len(ss) - 1) for j, s in enumerate(ss)],
+                dk + lks, (), [bn], dur=pe(2 * len(ss)), n=len(ss))
 
         def compare(bn, j, s):
             src, out = T[bn][:, big(j)], T.cc[:, :, 16 * s:16 * s + 16]
@@ -329,7 +331,11 @@ def rank_program(g, core, T, topo):
             else:
                 add("V", "cv", lambda: [V.tensor_scalar(out, src, T.kc[:, s:s + 1], None, OP.is_lt)], ["kc"], ["cc%d" % s], [bn], dur=vd(128))
         for bn, ss in places:
-            add("P", "pkr" + bn[2], krow(T[bn], ss), dk + lks + ["negv", "ones"], (), [bn], dur=pe(4 * len(ss)), n=1 + len(ss))
+            kconst(bn, len(ss))
+        add("P", "pkc", kcol, dk + ["negv", "ones", "r2" if k else "r1"], (), ["pa2"], dur=pe(3), n=2 if k else 5)
+        add("V", "kc", lambda: [V.tensor_copy(T.kc[:, :], pa2[:, 0:8])], (), ["kc"], ["pa2"], dur=vd(8))
+        for bn, ss in places:
+            krow(bn, ss)
         for bn, ss in places:
             for j, s in enumerate(ss):
                 compare(bn, j, s)
@@ -339,14 +345,24 @@ def rank_program(g, core, T, topo):
         else:
             add("P", "pq", lambda: [P.matmul(qr, kb["ql%d" % q], dq[q], q == 0, q == 3) for q in range(4)], dk + ["ql%d" % q for q in range(4)], (),
                 ["pb0"], dur=pe(8), n=4)
-        add("S", "sq_", lambda: [S.activation(T.src[:, 256:384], qr, AF.Copy)], (), ["srcq"], ["pb0"], dur=sd(128))
+        sq = add("S", "sq_", lambda: [S.activation(T.src[:, 256:384], qr, AF.Identity, bias=-2048.0)], (), ["srcq"], ["pb0"], dur=sd(128))
+        if k:
+            add("S", "sq_", lambda: [S.activation(T.qo[:, :], qr, AF.Copy)], (), ["qo"], ["pb0"], dur=sd(128), extra=[sq])
         add("P", "pl", lambda: [P.matmul(pa2[:, 8 + j:9 + j], T.cc[:, j, :], ones1, True, True) for j in range(8)],
             ["cc%d" % s for s in range(8)] + ["ones"], (), ["pa2"], dur=pe(8), n=8)
-        lists = [("scl2", "ad0"), ("scl2", "ad1"), ("scl1", "ad2")]
-        add("V", "po", lambda: [V.tensor_scalar(T.po[:, 8 * j:8 * j + 8], pa2[:, 8:16], cf[a], cf[b], OP.mult, OP.add) for j, (a, b) in enumerate(lists)],
-            ["scl2", "ad0", "ad1", "scl1", "ad2"], ["po"], ["pa2"], dur=3 * vd(8), n=3)
-        add("V", "scat", lambda: [V.tensor_copy(T.win[:, :].indirect(T.po[:, :]), T.src[:, :])], ["po", "srcA", "srcB", "srcq"], ["win"],
-            dur=50 + vd(384, 3.0))
+
+        def lists(sem, key, js, ab):
+            add("V", sem, lambda: [V.tensor_scalar(T.po[:, 8 * j:8 * j + 8], pa2[:, 8:16], cf[a], cf[b], OP.mult, OP.add) for j, (a, b) in zip(js, ab)],
+                [x for y in ab for x in y], [key], ["pa2"], dur=len(js) * vd(8), n=len(js))
+        lists("po", "po", (0, 1), [("scl2", "ad0"), ("scl2", "ad1")])
+        add("V", "scat", lambda: [V.tensor_copy(T.win[:, 0:256].indirect(T.po[:, 0:16]), T.src[:, 0:256])], ["po", "srcA", "srcB"], ["win"],
+            dur=50 + vd(256, 3.0))
+        for c in range(NC):
+            add("V", "nw%d" % c, (lambda w: lambda: [V.tensor_copy(T.wh[:, w], T.win[:, w])])(slice(64 * c, 64 * c + 64)), ["win"], ["wh%d" % c], dur=vd(64))
+        lists("poq", "poq", (2,), [("scl1", "ad2")])
+        add("V", "scq", lambda: [V.tensor_copy(T.win[:, 256:384].indirect(T.po[:, 16:24]), T.src[:, 256:384])], ["poq", "srcq"], ["winq"],
+            dur=50 + vd(128, 3.0))
+        add("V", "whq", lambda: [V.tensor_copy(T.wh[:, 256:384], T.win[:, 256:384])], ["winq"], ["whq"], dur=vd(128))
 
     def spap(c, t, st=1):
         return T.sp[:, 320 * c + 64 * (t - 1):320 * c + 64 * t:st]
@@ -367,23 +383,28 @@ def rank_program(g, core, T, topo):
         add("P", "pg" + C, fn, ["sg" + C, "dg%d" % t, "m16"] + ["sp%d_%d" % (c, u) for u in range(1, t)] + ["idh%d" % HS[u - 1] for u in range(1, t)]
             + (["i64b", "nt" + C] if t == 5 else []), (), ["pb" + C], dur=pe(n), n=n)
 
-    def start_chunk(k, c):
-        b, bk, o, W, C, K = T["pb%d" % c], ["pb%d" % c], 64 * c, T.win, str(c), str(k)
-        pm, dm, idf, dqp, w = kf["pm" + K], kf["dm" + K], kf["idf"], b[:, 320:384], slice(64 * c, 64 * c + 64)
-        add("P", "pD" + C, lambda: [P.matmul(b[:, 256:320:2], pm, W[:, o:o + 64:2], True, True),
-                                    P.matmul(b[:, 257:320:2], idf, W[:, o + 1:o + 64:2], True, True)], ["win", "pm" + K, "idf"], (), bk, dur=pe(8), n=2)
+    def first(k, c):
+        b, bk, o, W, C, K = T["pb%d" % c], ["pb%d" % c], 64 * c, T.wh, str(c), str(k)
+        add("P", "pD" + C, lambda: [P.matmul(b[:, 256:320:2], kh["pm" + K], W[:, o:o + 64:2], True, True),
+                                    P.matmul(b[:, 257:320:2], kh["idd"], W[:, o + 1:o + 64:2], True, True)],
+            ["wh" + C, "pm" + K, "idd"], (), bk, dur=pe(2), n=2)
         add("V", "x" + C, lambda: [V.tensor_copy(T.x[:, o:o + 64], b[:, 256:320])], (), ["x" + C], bk, dur=vd(64))
-        qw = slice(256 + 32 * c, 288 + 32 * c)
-        add("P", "pD" + C, lambda: [P.matmul(b[:, 128:192], dm, W[:, o:o + 64], True, True), P.matmul(b[:, 192:256], idf, W[:, o:o + 64], True, True),
+
+    def rest_of(k, c):
+        b, bk, o, W, C, K = T["pb%d" % c], ["pb%d" % c], 64 * c, T.wh, str(c), str(k)
+        dm, idd, dqp, w, qw = kh["dm" + K], kh["idd"], b[:, 320:384], slice(64 * c, 64 * c + 64), slice(256 + 32 * c, 288 + 32 * c)
+        add("P", "pD" + C, lambda: [P.matmul(b[:, 128:192], dm, W[:, w], True, True), P.matmul(b[:, 192:256], idd, W[:, w], True, True),
                                     P.matmul(b[:, 320:384:2], dm, W[:, qw], True, True), P.matmul(b[:, 321:384:2], dm, W[:, qw], True, True)],
-            ["win", "dm" + K, "idf"], (), bk, dur=pe(16), n=4)
+            ["wh" + C, "whq", "dm" + K, "idd"], (), bk, dur=pe(4), n=4)
         add("S", "sg" + C, lambda: [S.activation(T.sg[:, w], dqp, AF.Sign, bias=-0.5, scale=cf["nl" + K])], ["nl" + K], ["sg" + C], bk, dur=sd(64))
         add("V", "nt" + C, lambda: [V.tensor_scalar(T.nt[:, w], dqp, cf["th" + K], None, OP.is_le)], ["th" + K], ["nt" + C], bk, dur=vd(64))
 
     def trial(k, c, t, b1, b2):
         b, bk, a, o, C, K = T["pb%d" % c], ["pb%d" % c], T["pa%d" % c], 64 * c, str(c), str(k)
         w, w3, sp, h = slice(o, o + 64), slice(32 * c, 32 * c + 32), "sp%d_%d" % (c, t), "idh%d" % HS[t - 1]
-        measure(c, T.x, "x" + C, T.shs, slots, b1, b2)
+        measure(c, T.x, "x" + C, T.shs, slots, b1, b2, US)
+        if t == 1:
+            rest_of(k, c)
         pre_g(c, t)
         add("P", "pd" + C, lambda: [P.matmul(a[:, 128 + e:192:2], kb[n + K], ext(m, c), n == "sdp", n == "sdn")
                                     for e in (0, 1) for n, m in (("sdp", T.mx), ("sdn", T.mn))],
@@ -393,15 +414,16 @@ def rank_program(g, core, T, topo):
         add("V", "mk" + C, lambda: [V.tensor_scalar(T.mk[:, w], b[:, 64:128], 0.0, None, OP.is_equal)], (), ["mk" + C], bk, dur=vd(64))
         add("V", "md" + C, lambda: [V.tensor_tensor(T.md[:, w], T.mk[:, w], b[:, 128:192], OP.mult)], ["mk" + C], ["md" + C], bk, dur=vd(64))
         nm, dst = ("x", T.x) if t < 5 else ("nw", T.nw)
-        add("V", nm + C, lambda: [V.tensor_tensor(dst[:, w], T.md[:, w], b[:, 192:256], OP.add)], ["md" + C], [nm + C], bk, dur=vd(64))
+        add("V", nm + C, lambda: [V.tensor_tensor(dst[:, w], T.md[:, w], b[:, 192:256], OP.add)], ["md" + C],
+            [("x" if t < 5 else "new") + C], bk, dur=vd(64))
         if t == 5 and k == 0:
-            add("P", "fs" + C, lambda: [P.matmul(b[:, 448:480], kb["idh%d" % HS[u - 1]], spap(c, u, 2), u == 1, u == 5) for u in range(1, 6)],
+            add("P", "pD" + C, lambda: [P.matmul(b[:, 448:480], kb["idh%d" % HS[u - 1]], spap(c, u, 2), u == 1, u == 5) for u in range(1, 6)],
                 ["sp%d_%d" % (c, u) for u in range(1, 6)], (), bk, dur=pe(5), n=5)
             add("V", "pf" + C, lambda: [V.tensor_tensor(T.pf[:, w3], T.sg[:, o:o + 64:2], b[:, 448:480], OP.mult)], ["sg" + C], ["pf" + C], bk, dur=vd(32))
 
     def trials(k, b1, b2):
         for c in range(NC):
-            start_chunk(k, c)
+            first(k, c)
         for t in range(1, 6):
             for c in range(NC):
                 trial(k, c, t, b1, b2)
@@ -414,7 +436,7 @@ def rank_program(g, core, T, topo):
         ts("lk%d" % s, kb["lk%d" % s], kf["mrow"], "mrow r2f", 0.0, OP.mult, T.r2f[:, s:s + 1], OP.add)
     ts("sameb", kb["sameb"], kf["sm"], "sm ps", cf["ps"], OP.is_equal)
     round_consts(1)
-    nwk = ["nw%d" % c for c in range(NC)] + ["po"]
+    nwk = ["new%d" % c for c in range(NC)] + ["po"]
     add("S", "un1", lambda: [S.activation(T.src[:, 0:128], T.nw[:, :].indirect(T.po[:, 0:8]), AF.Copy)], nwk, ["srcA"], dur=sd(128, GR))
     add("V", "un2", lambda: [V.tensor_copy(T.src[:, 128:256], T.nw[:, :].indirect(T.po[:, 8:16]))], nwk, ["srcB"], dur=50 + vd(128, GR))
     add("V", "xo", lambda: [V.tensor_copy(T.xo[:, e:256:2], T.src[:, 128 * e:128 * e + 128]) for e in (0, 1)], ["srcA", "srcB"], xok, dur=2 * vd(128), n=2)
@@ -423,18 +445,18 @@ def rank_program(g, core, T, topo):
         ["nb1", "nb2"], dur=2 * vd(1), n=2)
     measure_all(T.shs, slots, "nb1", "nb2")
     order(1)
-    send(["srcq"], lambda q: T.src[:, 256:384], T.lq[:, big(r)], "aq", 3000)
-    arrive("aq", others, "lq", 90000.0)
+    s_q = send(["qo"], lambda q: T.qo[:, :], T.lq[:, big(r)], "aq")
+    arrive("aq", others, "lq", s_q, 6000.0)
 
     def yq():
         o = []
         for b in (0, 1):
             p = 32 * r + 16 * b
             for q in range(4):
-                s = T.src[p:p + 1, 256:384] if q == r else T.lq[p:p + 1, big(q)]
+                s = T.qo[p:p + 1, :] if q == r else T.lq[p:p + 1, big(q)]
                 o.append(g.sync.dma_start(T.yq[2 * q + b:2 * q + b + 1, :], s))
         return o
-    add("Y", "douq", yq, ["srcq", "lq"], ["yq"], dur=800, lat=2000, n=8, inc=16)
+    add("Y", "douq", yq, ["qo", "lq"], ["yq"], dur=800, lat=2000, n=8, inc=16)
     trials(1, "nb1", "nb2")
 
     add("S", "un1", lambda: [S.activation(T.ou[:, 0:256:2], T.nw[:, :].indirect(T.po[:, 0:8]), AF.Identity, bias=2048.0)], nwk, ["ouA"], dur=sd(128, GR))
@@ -448,11 +470,11 @@ def rank_program(g, core, T, topo):
     blocks = [(T.sto[32 * a:32 * a + 32, 64 * q:64 * q + 64], T.ou[rows(q), 64 * a:64 * a + 64]) for q in others for a in range(4)]
     copies("V", "x0", blocks[:7], ["ouA", "ouB"], "stoV")
     copies("S", "sq0", blocks[7:], ["ouA", "ouB"], "stoS")
-    send(["stoV", "stoS"], lambda q: T.sto[:, 64 * q:64 * q + 64], T.lr[:, 64 * r:64 * r + 64], "al%d" % r, 3000)
+    s_o = send(["stoV", "stoS"], lambda q: T.sto[:, 64 * q:64 * q + 64], T.lr[:, 64 * r:64 * r + 64], "al%d" % r)
     add("Y", "dou", lambda: [g.sync.dma_start(T.yu[rows(r), :], T.ou[rows(r), :])], ["ouA", "ouB"], ["yu"], dur=100, lat=2000, inc=16)
 
     def back(j, q):
-        arrive("al%d" % q, [q], "lr%d" % q, 1e6 + 1000.0 * j)
+        arrive("al%d" % q, [q], "lr%d" % q, s_o, 3000.0 + 500.0 * j)
         cps = [(T.yo[rows(q), 64 * a:64 * a + 64], T.lr[32 * a:32 * a + 32, 64 * q:64 * q + 64]) for a in range(4)]
         m = 3 if j < 2 else 2
         copies("V", "x1", cps[:m], ["lr%d" % q], "yoV%d" % q)
@@ -463,51 +485,66 @@ def rank_program(g, core, T, topo):
     return emit(T, dict(V=V, S=S, P=P, G=g, Y=g.sync), tasks, count)
 
 
-def stage(t):
-    return t["sem"].rstrip("0123456789")
+def place(tasks, pred, succ, key, back):
+    n = len(tasks)
+    need, st, busy = [len(p) for p in pred], [0.0] * n, {}
+    pool = set(i for i in range(n) if need[i] == 0)
+    while pool:
+        i = min(pool, key=lambda j: (key[j], j))
+        pool.discard(i)
+        t = tasks[i]
+        s, d = 0.0, t["dur"]
+        for p, hard in pred[i]:
+            s = max(s, st[p] + tasks[p]["dur"] + ((t if back else tasks[p])["lat"] + WAKE if hard else 0.0))
+        if t["eng"] != "R":
+            iv = busy.setdefault(t["eng"], [])
+            j = len(iv)
+            while j and iv[j - 1][1] > s:
+                j -= 1
+            while j < len(iv) and iv[j][0] < s + d - 0.001:
+                s = max(s, iv[j][1])
+                j += 1
+            iv.insert(j, (s, s + d))
+        st[i] = s
+        for q, _ in succ[i]:
+            need[q] -= 1
+            if need[q] == 0:
+                pool.add(q)
+    return st
+
+
+def bias(t):
+    x = t["sem"]
+    y = x.rstrip("0123456789")
+    return SB.get(y, 0.0) + (LB * (3 - int(x[len(y):])) if y != x and len(y) <= 2 and y in LANE else 0.0)
 
 
 def emit(T, E, tasks, count):
     n = len(tasks)
-    succ, soft, before = [[] for _ in range(n)], [[] for _ in range(n)], {}
+    pred, succ, before = [[] for _ in range(n)], [[] for _ in range(n)], {}
     for i, t in enumerate(tasks):
         if t["sem"] in before and tasks[before[t["sem"]]]["eng"] == t["eng"]:
             t["soft"].add(before[t["sem"]])
         before[t["sem"]] = i
-        for d in t["deps"]:
-            succ[d].append(i)
-        for d in t["soft"] - t["deps"]:
-            soft[d].append(i)
-    need = [len(t["deps"] | t["soft"]) for t in tasks]
-    rest, prio = [0.0] * n, [0.0] * n
+        for hard, ds in ((1, t["deps"]), (0, t["soft"] - t["deps"])):
+            for d in ds:
+                pred[i].append((d, hard))
+                succ[d].append((i, hard))
+    rest = [0.0] * n
     for i in range(n - 1, -1, -1):
-        t = tasks[i]
-        rest[i] = t["dur"] + t["lat"] + max([rest[j] + WAKE for j in succ[i]] or [0.0])
-        b = stage(t)
-        prio[i] = rest[i] + BIAS.get(b, 0.0) + (LANEB * (3 - int(t["sem"][len(b):])) if b != t["sem"] and len(b) <= 2 else 0.0)
-    look = [SCLA if stage(t) in ("mx", "mn") else GALA if stage(t) == "ga" else 0.0 for t in tasks]
-    est, fin, free, seq = [t["ready"] for t in tasks], [0.0] * n, {}, {}
-    pool = set(i for i in range(n) if need[i] == 0)
-    while pool:
-        best = None
-        for i in pool:
-            s = max(est[i], free.get(tasks[i]["eng"], 0.0))
-            key = (round((s + look[i]) / BUCKET), -prio[i], i)
-            if best is None or key < best[0]:
-                best = (key, i, s)
-        _, i, s = best
-        pool.discard(i)
-        t = tasks[i]
-        if t["eng"] != "R":
-            free[t["eng"]] = s + t["dur"]
-        seq.setdefault(t["eng"], []).append(i)
-        fin[i] = s + t["dur"] + t["lat"]
-        for j in succ[i]:
-            est[j] = max(est[j], fin[i] + WAKE)
-        for j in succ[i] + soft[i]:
-            need[j] -= 1
-            if need[j] == 0:
-                pool.add(j)
+        rest[i] = tasks[i]["dur"] + tasks[i]["lat"] + max([rest[j] + WAKE for j, h in succ[i] if h] or [0.0])
+    st = place(tasks, pred, succ, [-x - bias(t) for x, t in zip(rest, tasks)], False)
+    best = (1e18, None)
+    for k in range(ITERS + 1):
+        end = max(s + t["dur"] + t["lat"] for s, t in zip(st, tasks))
+        if end < best[0]:
+            best = (end, st)
+        if k < ITERS:
+            sb = place(tasks, succ, pred, [-(s + t["dur"]) for s, t in zip(st, tasks)], True)
+            st = place(tasks, pred, succ, [-(s + t["dur"]) for s, t in zip(sb, tasks)], False)
+    st, seq = best[1], {}
+    for i in sorted(range(n), key=lambda i: (st[i], i)):
+        seq.setdefault(tasks[i]["eng"], []).append(i)
     clocks, after = {e: {} for e in E}, [None] * n
     pos, left = {e: 0 for e in seq}, n
     while left:
@@ -520,7 +557,7 @@ def emit(T, E, tasks, count):
                     break
                 ck = clocks.get(e, {})
                 if e != "R":
-                    for d in sorted(t["deps"], key=lambda d: -fin[d]):
+                    for d in sorted(t["deps"], key=lambda d: -st[d]):
                         sem, val = tasks[d]["sem"], tasks[d]["val"]
                         if ck.get(sem, 0) < val:
                             E[e].wait_ge(T.sem[sem], int(val))
@@ -533,6 +570,7 @@ def emit(T, E, tasks, count):
                 pos[e] += 1
                 left -= 1
         assert left < was
-    for s in sorted(count):
+    last = {t["sem"]: s + t["dur"] + t["lat"] for s, t in zip(st, tasks)}
+    for s in sorted(count, key=lambda s: (last[s], s)):
         E["P"].wait_ge(T.sem[s], int(count[s]))
-    return seq, fin, tasks
+    return seq, st, tasks

from concourse.bass import DstId, RemoteDMATransfer
from concourse.mybir import dt, AluOpType as OP, AxisListType, ActivationFunctionType as AF

NC, CU = 4, 32
US, USM = 32, 24
BIG = 786432.0
HS = (16, 8, 4, 2, 1)
SFROM = 5
GR, VF, SFX, PEC, WAKE, ITERS = 1.56, 12.0, 65.0, 0.71, 110.0, 1
LB = 1200.0
SB = {"ga": -800.0, "mx": -800.0, "mn": -800.0, "mk": -800.0, "md": -800.0, "x": -800.0, "t": 800.0, "of": -800.0}

F32M = ["mrow", "sm", "im", "idf", "le", "same", "pmt", "e1", "e2"]
B16M = (["ineg", "i64b", "m16", "sameb", "ones", "sdp0", "sdn0", "sdp1", "sdn1", "lp0", "lp1", "ln0", "ln1"] + ["idh%d" % h for h in HS]
        + ["dg%d" % t for t in range(1, 6)] + ["lk%d" % s for s in range(8)] + ["ql%d" % q for q in range(4)])
H16M = ["tri", "onesb", "i64h", "idd", "pm0", "pm1", "dm0", "dm1"]
COLF = ["pcf", "ps", "pi", "b1", "b2", "nb1", "nb2", "asum", "lam0", "lam1", "px0", "px1", "psx0", "psx1", "th0", "th1", "nl0", "nl1",
        "va", "vb", "vv", "vt", "colr", "fc", "scl2", "ad0", "ad1", "scl1", "ad2"] + ["dc%d" % t for t in range(1, 6)]
COLI = ["pc", "psi", "ii", "odd", "bit0", "bit1"] + ["fi%d" % h for h in (8, 4, 2, 1)]
SCRATCH = {"cc": ("sbuf", [128, 8, 128], "bfloat16"), "st": ("dram", [512, 1024], "bfloat16"), "su": ("dram", [512, 64], "int32"),
           "lsh": ("dram", [512, 1024], "bfloat16"), "lu": ("dram", [512, 64], "int32")}
for _d, _l in (("float32", (("kf", 128 * len(F32M)), ("cf", len(COLF)), ("row8", 8), ("ind", 8), ("r2t", 8), ("r2f", 8), ("sq", 256), ("md", 256),
                            ("pf", 128), ("nw", 256), ("kc", 8), ("src", 384), ("win", 384), ("ou", 256), ("sto", 256), ("lr", 256), ("yo", 256),
                            ("qo", 128), ("lq", 512))),
               ("bfloat16", (("kb", 128 * len(B16M)), ("r1", 4), ("r2", 8), ("negv", 512), ("cl", 128), ("cr", 128), ("mmx", 1024), ("mmn", 1024),
                             ("sh0", 4096), ("shs", 4096), ("y", 256), ("ga", 4096), ("mx", 4096), ("mn", 4096), ("mk", 256), ("sp", 1280),
                             ("sg", 256), ("nt", 256), ("dd", 128), ("dl", 512))),
               ("float16", (("kh", 128 * len(H16M)), ("xo", 256), ("x", 256), ("wh", 384))),
               ("int32", (("ci", len(COLI)), ("un0", 256), ("uns", 256), ("t3", 256), ("sf", 256))),
               ("uint16", (("of", 256), ("po", 24)))):
    for _n, _w in _l:
        SCRATCH[_n] = ("sbuf", [128, _w], _d)
for _i in range(4):
    SCRATCH["pa%d" % _i] = ("psum", [128, 512], "float32")
    SCRATCH["pb%d" % _i] = ("psum", [128, 512], "float32")
LANE = "pw px y py sq t sf of ga gv mx mn pd sp pg pc mk md x pD sg nt nw pf dd".split()
ONE = ("vk gk srcu xo pkc kc pk0 pk1 pk3 pkr0 pkr1 pkr3 cv cs pq sq_ pl po poq scat scq whq red un1 un2 dst dsu dun dsh dut douq dou "
       "au ad aq loc").split()
SEMAPHORES = [s + str(c) for s in LANE for c in range(NC)] + ONE + [s + str(q) for s in ("ash", "bs", "al") for q in range(4)]


def vd(n, rate=1.0):
    return max(64.0, n * rate) * 0.83 + VF


def sd(n, rate=1.0):
    return max(64.0, n * rate) * 0.83 + SFX


def pe(n):
    return n * (64 * PEC) + 10.0


def rank_program(g, core, T, topo):
    r = T.rank_of(core)
    if r is None:
        return
    cores = list(T.cores)
    others = [q for q in range(4) if q != r]
    V, S, P = g.vector, g.scalar, g.tensor
    tasks, lastw, readers, bank, count = [], {}, {}, {}, {}

    def add(eng, sem, fn, reads=(), writes=(), banks=(), dur=60.0, lat=0.0, n=1, inc=1, extra=()):
        i = len(tasks)
        deps, soft = set(extra), set()
        for k in list(reads) + list(writes):
            if k in lastw:
                deps.add(lastw[k])
        for k in writes:
            deps.update(readers.get(k, ()))
        for b in banks:
            st = bank.setdefault(b, {})
            for e in [e for e in st if e != eng]:
                deps.update(st.pop(e))
            if eng in st:
                soft.add(st[eng][-1])
            st.setdefault(eng, []).append(i)
        for k in reads:
            readers.setdefault(k, []).append(i)
        for k in writes:
            lastw[k] = i
            readers[k] = []
        count[sem] = count.get(sem, 0) + n * inc
        tasks.append(dict(eng=eng, sem=sem, val=count[sem], inc=inc, fn=fn, deps=deps, soft=soft - deps, dur=dur, lat=lat))
        return i

    def mats(buf, names):
        return {n: buf[:, 128 * i:128 * i + 128] for i, n in enumerate(names)}
    kf, kb, kh = mats(T.kf, F32M), mats(T.kb, B16M), mats(T.kh, H16M)
    cf = {n: T.cf[:, i:i + 1] for i, n in enumerate(COLF)}
    ci = {n: T.ci[:, i:i + 1] for i, n in enumerate(COLI)}
    ob = B16M.index("ones") * 128
    ones1, onesrow, ones8 = T.kb[:, ob:ob + 1], T.kb[0:1, ob:ob + 128], T.kb[0:1, ob:ob + 8]

    def rows(q):
        return slice(32 * q, 32 * q + 32)

    def big(q):
        return slice(128 * q, 128 * q + 128)
    add("S", "dun", lambda: [S.dma_start(T.un0[:, :], T.units[:, :])], (), ["un0"], dur=100, lat=2000, inc=16)
    add("Y", "dst", lambda: [g.sync.dma_start(T.st[big(q), :], T.shelf[rows(q), :]) for q in others], (), ["st"], dur=300, lat=4000, n=3, inc=16)
    add("S", "dsu", lambda: [S.dma_start(T.su[big(q), :], T.units[rows(q), :]) for q in others], (), ["su"], dur=300, lat=2000, n=3, inc=16)
    add("Y", "dsh", lambda: [g.sync.dma_start(T.sh0[:, :], T.shelf[:, :])], (), ["sh0"], dur=100, lat=7000, inc=16)
    add("Y", "bs%d" % r, lambda: [g.sync.dma_start(T.shs[rows(r), :], T.shelf[rows(r), :])], (), ["shs%d" % r], dur=100, lat=8000, inc=16)

    def split(p):
        oth = [q for q in range(4) if q != p]
        away = [q for q in oth if (topo.host(cores[q]), topo.chip(cores[q])) != (topo.host(cores[p]), topo.chip(cores[p]))]
        offe = topo.engines(cores[p], cores[away[0]])
        w = len(offe) // len(away)
        res = {q: offe[k * w:k * w + w] for k, q in enumerate(away)}
        for q in oth:
            if q not in away:
                res[q] = [e for e in topo.engines(cores[p], cores[q]) if e not in offe]
        return res, away
    eng_of, off = split(r)
    near = [q for q in others if q not in off]

    def send(reads, src_of, dst, sem):
        def fn():
            tr = []
            for q in others:
                rid, pid = topo.addr(cores[q], core)
                tr.append(RemoteDMATransfer(dst_ids=[DstId(rid=rid, pnc=pid)], dma_engine_mask=sum(1 << e for e in eng_of[q]),
                                            remote_sem=T.sem[sem], src=src_of(q), dst=dst))
            g.remote_dma_fused(tr, local_sem=T.sem["loc"])
            return []
        return add("G", "loc", fn, reads, (), dur=1500, n=sum(len(eng_of[q]) for q in others))

    def arrive(sem, qs, key, like, lat):
        add("R", sem, None, (), [key], dur=0.0, lat=lat, n=sum(len(split(q)[0][r]) for q in qs), extra=[like])

    prev = {}

    def const(eng, sem, fn, reads, key, dur):
        prev[sem] = add(eng, sem, lambda: [fn()], reads, [key], dur=dur, extra=[prev[sem]] if sem in prev else [])

    def iota(key, out, pattern, cm, n, **kw):
        const("G", "gk", lambda: g.iota(out, pattern, 0, cm, **kw), [], key, 130 + 1.66 * n)

    def ts(key, out, in0, rk, s1, op0, s2=None, op1=None, n=128):
        a = (out, in0, s1, None, op0) if op1 is None else (out, in0, s1, s2, op0, op1)
        const("V", "vk", lambda: V.tensor_scalar(*a), rk.split(), key, vd(n))

    def tc(name, in0, rk, *a):
        ts(name, cf[name] if name in cf else ci[name], (cf[in0] if in0 in cf else ci[in0]), in0 + " " + rk, *a, n=1)

    def tt(key, out, a, b, rk, op):
        const("V", "vk", lambda: V.tensor_tensor(out, a, b, op), rk.split(), key, vd(256))

    def ms(key, ap, v, n):
        const("V", "vk", lambda: V.memset(ap, v), [], key, vd(n, 0.5))

    def diag(name, out, v, rk=""):
        ts(name, out, kf["mrow"], "mrow pcf " + rk, cf["pcf"], OP.is_equal, v, OP.mult)
    small = dict(allow_small_or_imprecise_dtypes=True)
    iota("pc", ci["pc"], [[0, 1]], 1, 1)
    iota("mrow", kf["mrow"], [[1, 128]], 0, 128, **small)
    iota("sm", kf["sm"], [[1, 8], [0, 16]], 0, 128, **small)
    iota("im", kf["im"], [[0, 8], [1, 16]], 0, 128, **small)
    ms("cl", T.cl[:, :], -512.0, 128)
    ms("cr", T.cr[:, 0:64], 0.0, 64)
    ms("cr", T.cr[:, 64:128], 256.0, 64)
    tc("pcf", "pc", "", 1.0, OP.mult)
    tc("psi", "pc", "", 4, OP.arith_shift_right)
    tc("ii", "pc", "", 15, OP.bitwise_and)
    tc("odd", "pc", "", 1, OP.bitwise_and)
    tc("ps", "psi", "", 1.0, OP.mult)
    tc("pi", "ii", "", 1.0, OP.mult)
    tc("b1", "odd", "", -2048.0, OP.mult, BIG + 2048.0 - 2047.5, OP.add)
    tc("b2", "odd", "", -2048.0, OP.mult, BIG + 2048.0, OP.add)
    ts("same", kf["same"], kf["sm"], "sm ps", cf["ps"], OP.is_equal)
    ts("le", kf["le"], kf["im"], "im pi", cf["pi"], OP.is_ge)
    tt("tri", kh["tri"], kf["same"], kf["le"], "same le", OP.mult)
    ts("onesb", kh["onesb"], kf["sm"], "sm ps", cf["ps"], OP.is_equal)
    xok = ["xo%d" % c for c in range(NC)]
    add("V", "xo", lambda: [V.tensor_scalar(T.xo[:, :], T.un0[:, :], -2048.0, None, OP.add)], ["un0"], xok, dur=vd(256))
    diag("ineg", kb["ineg"], -1.0)
    diag("i64h", kh["i64h"], 64.0)
    ms("mmx", T.mmx[:, :], 0.0, 1024)
    ms("mmx", T.mmx[:, 0:1024:32], -512.0, 32)
    ms("mmn", T.mmn[:, :], 0.0, 1024)
    ms("mmn", T.mmn[:, 0:1024:32], 512.0, 32)

    s_u = send(["su"], lambda q: T.su[big(q), :], T.lu[big(r), :], "au")
    s_s = send(["st"], lambda q: T.st[big(q), :], T.lsh[big(r), :], "ash%d" % r)
    iota("row8", T.row8[:, :], [[1, 8]], 0, 8, **small)
    iota("negv", T.negv[0:1, :], [[0, 4], [-1, 128]], 0, 512, **small)
    arrive("au", others, "lu", s_u, 3500.0)
    add("Y", "dut", lambda: [g.sync.dma_start(T.uns[rows(q), :], T.units[rows(r), :] if q == r else T.lu[big(q), :]) for q in range(4)],
        ["lu"], ["uns"], dur=400, lat=2000, n=4, inc=16)

    def bounce(q):
        arrive("ash%d" % q, [q], "lsh%d" % q, s_s, 6000.0 if q in near else 10000.0)
        add("Y", "bs%d" % q, lambda: [g.sync.dma_start(T.shs[rows(q), :], T.lsh[big(q), :])], ["lsh%d" % q], ["shs%d" % q], dur=100, lat=3000, inc=16)
    for q in near + off:
        bounce(q)
    slots = ["shs%d" % q for q in range(4)]

    def measure(c, xb, xkey, shelf, skeys, b1, b2, us):
        a, bk, b, o, v = T["pa%d" % c], ["pa%d" % c], T["pb%d" % c], 64 * c, 1024 * c
        X, X0, X1, XY = a[:, 0:128], a[:, 0:64], a[:, 64:128], b[:, 384:448]
        C = str(c)
        w, wo = slice(o, o + 64), slice(o, o + 64, 2)
        add("P", "pw" + C, lambda: [P.matmul(XY, kh["tri"], xb[:, w], True, False), P.matmul(b[:, 385:448:2], kh["onesb"], xb[:, wo], False, True)],
            [xkey, "tri", "onesb"], (), ["pb" + C], dur=pe(2), n=2)
        add("V", "y" + C, lambda: [V.tensor_scalar(T.y[:, w], XY, cf[b1], None, OP.add)], [b1], ["y" + C], ["pb" + C], dur=vd(64))
        add("P", "px" + C, lambda: [P.matmul(X, T.cl[0:1, :], T.cr[0:1, :], True, False), P.matmul(X1, kh["i64h"], xb[:, w], False, False),
                                    P.matmul(X0, kh["tri"], xb[:, w], False, False), P.matmul(a[:, 1:64:2], kh["onesb"], xb[:, wo], False, False)],
            [xkey, "tri", "onesb", "cl", "cr", "i64h"], (), bk, dur=pe(5), n=4)
        add("P", "py" + C, lambda: [P.matmul(X0, kb["ineg"], T.y[:, w], False, True)], ["y" + C, "ineg"], (), bk, dur=pe(1))
        add("S", "sq" + C, lambda: [S.activation(T.sq[:, w], X0, AF.Square, bias=cf[b2])], [b2], ["sq" + C], bk, dur=sd(64))
        add("V", "t" + C, lambda: [V.tensor_tensor(T.t3[:, w], T.sq[:, w], X1, OP.add)], ["sq" + C], ["t3" + C], bk, dur=vd(64))
        add("V", "sf" + C, lambda: [V.tensor_scalar(T.sf[:, w], T.t3[:, w], 6, 4095, OP.arith_shift_right, OP.bitwise_and)], ["t3" + C], ["sf" + C],
            dur=vd(64))
        add("V", "of" + C, lambda: [V.tensor_copy(T.of[:, w], T.sf[:, w])], ["sf" + C], ["of" + C], dur=vd(64))
        m = v + 32 * us
        add("S", "ga" + C, lambda: [S.activation(T.ga[:, v:m], shelf[:, :].indirect(T.of[:, o:o + 2 * us]), AF.Copy)],
            ["of" + C] + skeys, ["gas" + C], dur=sd(32 * us, GR))
        gk = ["gas" + C]
        if us < CU:
            gk.append("gav" + C)
            add("V", "gv" + C, lambda: [V.tensor_copy(T.ga[:, m:v + 1024], shelf[:, :].indirect(T.of[:, o + 2 * us:o + 64]))],
                ["of" + C] + skeys, ["gav" + C], dur=50 + vd(32 * (CU - us), GR))
        z = slice(v, v + 1024)
        gr = ["gas" + C, "gav" + C]
        add("V", "mx" + C, lambda: [V.tensor_tensor_scan(T.mx[:, z], T.mmx[:, :], T.ga[:, z], 0.0, OP.add, OP.max)], gr + ["mmx"], ["mx" + C],
            dur=vd(1024, 0.5))
        add("V", "mn" + C, lambda: [V.tensor_tensor_scan(T.mn[:, z], T.mmn[:, :], T.ga[:, z], 0.0, OP.add, OP.min)], gr + ["mmn"], ["mn" + C],
            dur=vd(1024, 0.5))

    def ext(buf, c):
        return buf[:, 1024 * c + 31:1024 * c + 1024:32]

    def measure_all(shelf, skeys, b1, b2):
        for c in range(NC):
            measure(c, T.xo, "xo%d" % c, shelf, skeys, b1, b2, USM)
            add("V", "dd%d" % c, (lambda c: lambda: [V.tensor_tensor(T.dd[:, 32 * c:32 * c + 32], ext(T.mx, c), ext(T.mn, c), OP.subtract)])(c),
                ["mx%d" % c, "mn%d" % c], ["dd%d" % c], dur=vd(64))
    measure_all(T.sh0, ["sh0"], "b1", "b2")

    ms("ones", kb["ones"], 1.0, 128)
    ts("ind", T.ind[:, :], T.row8[:, :], "row8 ps", cf["ps"], OP.is_equal, 128.0, OP.mult, n=8)
    ts("r1", T.r1[:, 0:2], T.ind[:, 2 * r:2 * r + 2], "ind", 1.0, OP.mult, n=2)
    ts("r1", T.r1[:, 2:4], T.ind[:, 2 * r:2 * r + 2], "ind", -1.0, OP.mult, n=2)
    for b in (0, 1):
        ts("lp%d" % b, kb["lp%d" % b], kf["mrow"], "mrow ind", 0.0, OP.mult, T.ind[:, 2 * r + b:2 * r + b + 1], OP.add)
        ts("ln%d" % b, kb["ln%d" % b], kb["lp%d" % b], "lp%d" % b, -1.0, OP.mult)
    tc("va", "ps", "", float(2 * r), OP.is_ge)
    tc("vb", "ps", "", float(2 * r + 1), OP.is_le)
    tc("vv", "va", "vb", cf["vb"], OP.mult)
    tc("vt", "ps", "", float(100 - 2 * r), OP.add)
    tc("colr", "vt", "vv", cf["vv"], OP.mult, -100.0, OP.add)
    for q in range(4):
        ts("ql%d" % q, kb["ql%d" % q], kf["sm"], "sm colr", float(2 * q), OP.subtract, cf["colr"], OP.is_equal)
    tc("fc", "ps", "", float(SFROM), OP.is_ge)
    tc("scl2", "fc", "", -1.0, OP.mult, 2.0, OP.add)
    tc("ad0", "fc", "", 127.0, OP.mult)
    tc("ad1", "fc", "", 127.0, OP.mult, 1.0, OP.add)
    tc("scl1", "fc", "", -0.5, OP.mult, 1.0, OP.add)
    tc("ad2", "fc", "", 63.5, OP.mult)
    ms("win", T.win[:, 0:256], 0.0, 512)
    ms("winq", T.win[:, 256:384], 0.0, 256)
    for k, sh in ((0, 6), (1, 5)):
        tc("bit%d" % k, "pc", "", sh, OP.arith_shift_right, 1, OP.bitwise_and)
        tc("lam%d" % k, "bit%d" % k, "", -2.0, OP.mult, 1.0, OP.add)
    diag("idf", kf["idf"], 1.0)
    diag("idd", kh["idd"], 1.0)

    def round_consts(k):
        K = str(k)
        tc("px" + K, "lam" + K, "pcf", (64.0, 32.0)[k], OP.mult, cf["pcf"], OP.add)
        ts("pm" + K, kh["pm" + K], kf["mrow"], "mrow px" + K, cf["px" + K], OP.is_equal)
        ts("pmt", kf["pmt"], kf["mrow"], "mrow px" + K, cf["px" + K], OP.is_equal)
        tt("dm" + K, kh["dm" + K], kf["pmt"], kf["idf"], "idf pmt", OP.subtract)
        tc("nl" + K, "lam" + K, "", -1.0, OP.mult)
        tc("th" + K, "lam" + K, "", 0.5, OP.mult)
        tc("psx" + K, "lam" + K, "ps", (4.0, 2.0)[k], OP.mult, cf["ps"], OP.add)
        ts("e1", kf["e1"], kf["sm"], "sm ps lam" + K, cf["ps"], OP.is_equal, cf["lam" + K], OP.mult)
        ts("e2", kf["e2"], kf["sm"], "sm psx%s lam%s" % (K, K), cf["psx" + K], OP.is_equal, cf["lam" + K], OP.mult)
        tt("sdp" + K, kb["sdp" + K], kf["e1"], kf["e2"], "e1 e2", OP.add)
        ts("sdn" + K, kb["sdn" + K], kb["sdp" + K], "sdp" + K, -1.0, OP.mult)
    round_consts(0)
    diag("m16", kb["m16"], -16.0)
    for t in range(1, 6):
        h = HS[t] if t < 5 else 1
        if t < 5:
            tc("fi%d" % h, "pc", "", 16 - h, OP.bitwise_and)
        tc("dc%d" % t, "fi%d" % h, "", -1.0, OP.mult, 16.0 - h if t < 5 else 15.5, OP.add)
        diag("dg%d" % t, kb["dg%d" % t], cf["dc%d" % t], "dc%d" % t)
        diag("idh%d" % HS[t - 1], kb["idh%d" % HS[t - 1]], float(HS[t - 1]))
    diag("i64b", kb["i64b"], 64.0)

    dkeys = ["dd%d" % c for c in range(NC)]
    s_d = send(dkeys, lambda q: T.dd[:, :], T.dl[:, big(r)], "ad")
    arrive("ad", others, "dl", s_d, 3500.0)
    add("V", "srcu", lambda: [V.tensor_scalar(T.src[:, 128 * e:128 * e + 128], T.uns[:, e:256:2], -2048.0, None, OP.add) for e in (0, 1)],
        ["uns"], ["srcA", "srcB"], dur=2 * vd(128), n=2)

    def order(k):
        pa2 = T.pa2
        dq = [T.dd[:, :] if q == r or k else T.dl[:, big(q)] for q in range(4)]
        dk = dkeys + ([] if k else ["dl"])
        lks = ["lk%d" % s for s in range(8)] if k else ["lp0", "lp1", "ln0", "ln1"]

        def lk(s):
            return kb["lk%d" % s] if k else kb[("lp%d" if s < 4 else "ln%d") % (s % 2)]

        def kcol():
            o = [P.matmul(pa2[:, 0:8], T.negv[0:1, 0:128], ones8, True, False)]
            if k:
                return o + [P.matmul(pa2[:, 0:8], T.dd[:, :], T.r2[:, :], False, True)]
            for q in range(4):
                w = 0 if q < 2 else 2
                o.append(P.matmul(pa2[:, 2 * q:2 * q + 2], dq[q], T.r1[:, w:w + 2], False, q == 3))
            return o
        places = [("pa0", list(range(0, 4))), ("pa1", list(range(SFROM, 8))), ("pa3", list(range(4, SFROM)))]

        def kconst(bn, n):
            add("P", "pk" + bn[2], lambda: [P.matmul(T[bn][:, 0:128 * n], onesrow, T.negv[0:1, 0:128 * n], True, False)], ["negv", "ones"], (), [bn],
                dur=pe(2 * n))

        def krow(bn, ss):
            add("P", "pkr" + bn[2], lambda: [P.matmul(T[bn][:, big(j)], lk(s), dq[s // 2], False, j == len(ss) - 1) for j, s in enumerate(ss)],
                dk + lks, (), [bn], dur=pe(2 * len(ss)), n=len(ss))

        def compare(bn, j, s):
            src, out = T[bn][:, big(j)], T.cc[:, :, 16 * s:16 * s + 16]
            if bn == "pa1":
                add("S", "cs", lambda: [S.activation(out, src, AF.Sign, bias=T.kc[:, s:s + 1], scale=-1.0)], ["kc"], ["cc%d" % s], [bn], dur=sd(128))
            else:
                add("V", "cv", lambda: [V.tensor_scalar(out, src, T.kc[:, s:s + 1], None, OP.is_lt)], ["kc"], ["cc%d" % s], [bn], dur=vd(128))
        for bn, ss in places:
            kconst(bn, len(ss))
        add("P", "pkc", kcol, dk + ["negv", "ones", "r2" if k else "r1"], (), ["pa2"], dur=pe(3), n=2 if k else 5)
        add("V", "kc", lambda: [V.tensor_copy(T.kc[:, :], pa2[:, 0:8])], (), ["kc"], ["pa2"], dur=vd(8))
        for bn, ss in places:
            krow(bn, ss)
        for bn, ss in places:
            for j, s in enumerate(ss):
                compare(bn, j, s)
        qr = T.pb0[:, 0:128]
        if k:
            add("P", "pq", lambda: [P.matmul(qr, kb["sameb"], T.dd[:, :], True, True)], dk + ["sameb"], (), ["pb0"], dur=pe(2))
        else:
            add("P", "pq", lambda: [P.matmul(qr, kb["ql%d" % q], dq[q], q == 0, q == 3) for q in range(4)], dk + ["ql%d" % q for q in range(4)], (),
                ["pb0"], dur=pe(8), n=4)
        sq = add("S", "sq_", lambda: [S.activation(T.src[:, 256:384], qr, AF.Identity, bias=-2048.0)], (), ["srcq"], ["pb0"], dur=sd(128))
        if k:
            add("S", "sq_", lambda: [S.activation(T.qo[:, :], qr, AF.Copy)], (), ["qo"], ["pb0"], dur=sd(128), extra=[sq])
        add("P", "pl", lambda: [P.matmul(pa2[:, 8 + j:9 + j], T.cc[:, j, :], ones1, True, True) for j in range(8)],
            ["cc%d" % s for s in range(8)] + ["ones"], (), ["pa2"], dur=pe(8), n=8)

        def lists(sem, key, js, ab):
            add("V", sem, lambda: [V.tensor_scalar(T.po[:, 8 * j:8 * j + 8], pa2[:, 8:16], cf[a], cf[b], OP.mult, OP.add) for j, (a, b) in zip(js, ab)],
                [x for y in ab for x in y], [key], ["pa2"], dur=len(js) * vd(8), n=len(js))
        lists("po", "po", (0, 1), [("scl2", "ad0"), ("scl2", "ad1")])
        add("V", "scat", lambda: [V.tensor_copy(T.win[:, 0:256].indirect(T.po[:, 0:16]), T.src[:, 0:256])], ["po", "srcA", "srcB"], ["win"],
            dur=50 + vd(256, 3.0))
        for c in range(NC):
            add("V", "nw%d" % c, (lambda w: lambda: [V.tensor_copy(T.wh[:, w], T.win[:, w])])(slice(64 * c, 64 * c + 64)), ["win"], ["wh%d" % c], dur=vd(64))
        lists("poq", "poq", (2,), [("scl1", "ad2")])
        add("V", "scq", lambda: [V.tensor_copy(T.win[:, 256:384].indirect(T.po[:, 16:24]), T.src[:, 256:384])], ["poq", "srcq"], ["winq"],
            dur=50 + vd(128, 3.0))
        add("V", "whq", lambda: [V.tensor_copy(T.wh[:, 256:384], T.win[:, 256:384])], ["winq"], ["whq"], dur=vd(128))

    def spap(c, t, st=1):
        return T.sp[:, 320 * c + 64 * (t - 1):320 * c + 64 * t:st]

    def pre_g(c, t):
        C, w, b = str(c), slice(64 * c, 64 * c + 64), T["pb%d" % c]
        G = b[:, 64:128]

        def fn():
            o = [P.matmul(G, kb["dg%d" % t], T.sg[:, w], True, False),
                 P.matmul(b[:, 65:128:2], kb["m16"], T.sg[:, 64 * c + 1:64 * c + 64:2], False, False)]
            for u in range(1, t):
                o.append(P.matmul(G, kb["idh%d" % HS[u - 1]], spap(c, u), False, False))
            if t == 5:
                o.append(P.matmul(G, kb["i64b"], T.nt[:, w], False, False))
            return o
        n = t + 1 + (1 if t == 5 else 0)
        add("P", "pg" + C, fn, ["sg" + C, "dg%d" % t, "m16"] + ["sp%d_%d" % (c, u) for u in range(1, t)] + ["idh%d" % HS[u - 1] for u in range(1, t)]
            + (["i64b", "nt" + C] if t == 5 else []), (), ["pb" + C], dur=pe(n), n=n)

    def first(k, c):
        b, bk, o, W, C, K = T["pb%d" % c], ["pb%d" % c], 64 * c, T.wh, str(c), str(k)
        add("P", "pD" + C, lambda: [P.matmul(b[:, 256:320:2], kh["pm" + K], W[:, o:o + 64:2], True, True),
                                    P.matmul(b[:, 257:320:2], kh["idd"], W[:, o + 1:o + 64:2], True, True)],
            ["wh" + C, "pm" + K, "idd"], (), bk, dur=pe(2), n=2)
        add("V", "x" + C, lambda: [V.tensor_copy(T.x[:, o:o + 64], b[:, 256:320])], (), ["x" + C], bk, dur=vd(64))

    def rest_of(k, c):
        b, bk, o, W, C, K = T["pb%d" % c], ["pb%d" % c], 64 * c, T.wh, str(c), str(k)
        dm, idd, dqp, w, qw = kh["dm" + K], kh["idd"], b[:, 320:384], slice(64 * c, 64 * c + 64), slice(256 + 32 * c, 288 + 32 * c)
        add("P", "pD" + C, lambda: [P.matmul(b[:, 128:192], dm, W[:, w], True, True), P.matmul(b[:, 192:256], idd, W[:, w], True, True),
                                    P.matmul(b[:, 320:384:2], dm, W[:, qw], True, True), P.matmul(b[:, 321:384:2], dm, W[:, qw], True, True)],
            ["wh" + C, "whq", "dm" + K, "idd"], (), bk, dur=pe(4), n=4)
        add("S", "sg" + C, lambda: [S.activation(T.sg[:, w], dqp, AF.Sign, bias=-0.5, scale=cf["nl" + K])], ["nl" + K], ["sg" + C], bk, dur=sd(64))
        add("V", "nt" + C, lambda: [V.tensor_scalar(T.nt[:, w], dqp, cf["th" + K], None, OP.is_le)], ["th" + K], ["nt" + C], bk, dur=vd(64))

    def trial(k, c, t, b1, b2):
        b, bk, a, o, C, K = T["pb%d" % c], ["pb%d" % c], T["pa%d" % c], 64 * c, str(c), str(k)
        w, w3, sp, h = slice(o, o + 64), slice(32 * c, 32 * c + 32), "sp%d_%d" % (c, t), "idh%d" % HS[t - 1]
        measure(c, T.x, "x" + C, T.shs, slots, b1, b2, US)
        if t == 1:
            rest_of(k, c)
        pre_g(c, t)
        add("P", "pd" + C, lambda: [P.matmul(a[:, 128 + e:192:2], kb[n + K], ext(m, c), n == "sdp", n == "sdn")
                                    for e in (0, 1) for n, m in (("sdp", T.mx), ("sdn", T.mn))],
            ["mx" + C, "mn" + C, "sdp" + K, "sdn" + K], (), ["pa" + C], dur=pe(4), n=4)
        add("V", "sp" + C, lambda: [V.tensor_scalar(spap(c, t), a[:, 128:192], 0.0, -0.5, OP.is_gt, OP.add)], (), [sp], ["pa" + C], dur=vd(64))
        add("P", "pc" + C, lambda: [P.matmul(b[:, 64:128], kb[h], spap(c, t), False, True)], [sp, h], (), bk, dur=pe(1))
        add("V", "mk" + C, lambda: [V.tensor_scalar(T.mk[:, w], b[:, 64:128], 0.0, None, OP.is_equal)], (), ["mk" + C], bk, dur=vd(64))
        add("V", "md" + C, lambda: [V.tensor_tensor(T.md[:, w], T.mk[:, w], b[:, 128:192], OP.mult)], ["mk" + C], ["md" + C], bk, dur=vd(64))
        nm, dst = ("x", T.x) if t < 5 else ("nw", T.nw)
        add("V", nm + C, lambda: [V.tensor_tensor(dst[:, w], T.md[:, w], b[:, 192:256], OP.add)], ["md" + C],
            [("x" if t < 5 else "new") + C], bk, dur=vd(64))
        if t == 5 and k == 0:
            add("P", "pD" + C, lambda: [P.matmul(b[:, 448:480], kb["idh%d" % HS[u - 1]], spap(c, u, 2), u == 1, u == 5) for u in range(1, 6)],
                ["sp%d_%d" % (c, u) for u in range(1, 6)], (), bk, dur=pe(5), n=5)
            add("V", "pf" + C, lambda: [V.tensor_tensor(T.pf[:, w3], T.sg[:, o:o + 64:2], b[:, 448:480], OP.mult)], ["sg" + C], ["pf" + C], bk, dur=vd(32))

    def trials(k, b1, b2):
        for c in range(NC):
            first(k, c)
        for t in range(1, 6):
            for c in range(NC):
                trial(k, c, t, b1, b2)
    order(0)
    trials(0, "b1", "b2")
    ts("r2t", T.r2t[:, :], T.row8[:, :], "row8 ps lam1", cf["ps"], OP.is_equal, cf["lam1"], OP.mult, n=8)
    ts("r2f", T.r2f[:, :], T.r2t[:, :], "r2t", 128.0, OP.mult, n=8)
    ts("r2", T.r2[:, :], T.r2t[:, :], "r2t", 128.0, OP.mult, n=8)
    for s in range(8):
        ts("lk%d" % s, kb["lk%d" % s], kf["mrow"], "mrow r2f", 0.0, OP.mult, T.r2f[:, s:s + 1], OP.add)
    ts("sameb", kb["sameb"], kf["sm"], "sm ps", cf["ps"], OP.is_equal)
    round_consts(1)
    nwk = ["new%d" % c for c in range(NC)] + ["po"]
    add("S", "un1", lambda: [S.activation(T.src[:, 0:128], T.nw[:, :].indirect(T.po[:, 0:8]), AF.Copy)], nwk, ["srcA"], dur=sd(128, GR))
    add("V", "un2", lambda: [V.tensor_copy(T.src[:, 128:256], T.nw[:, :].indirect(T.po[:, 8:16]))], nwk, ["srcB"], dur=50 + vd(128, GR))
    add("V", "xo", lambda: [V.tensor_copy(T.xo[:, e:256:2], T.src[:, 128 * e:128 * e + 128]) for e in (0, 1)], ["srcA", "srcB"], xok, dur=2 * vd(128), n=2)
    add("V", "red", lambda: [V.tensor_reduce(cf["asum"], T.pf[:, :], AxisListType.X, OP.add)], ["pf%d" % c for c in range(NC)], ["asum"], dur=vd(128))
    add("V", "red", lambda: [V.tensor_scalar(cf["nb" + e], cf["asum"], cf["b" + e], 1984.0, OP.add, OP.add) for e in "12"], ["asum", "b1", "b2"],
        ["nb1", "nb2"], dur=2 * vd(1), n=2)
    measure_all(T.shs, slots, "nb1", "nb2")
    order(1)
    s_q = send(["qo"], lambda q: T.qo[:, :], T.lq[:, big(r)], "aq")
    arrive("aq", others, "lq", s_q, 6000.0)

    def yq():
        o = []
        for b in (0, 1):
            p = 32 * r + 16 * b
            for q in range(4):
                s = T.qo[p:p + 1, :] if q == r else T.lq[p:p + 1, big(q)]
                o.append(g.sync.dma_start(T.yq[2 * q + b:2 * q + b + 1, :], s))
        return o
    add("Y", "douq", yq, ["qo", "lq"], ["yq"], dur=800, lat=2000, n=8, inc=16)
    trials(1, "nb1", "nb2")

    add("S", "un1", lambda: [S.activation(T.ou[:, 0:256:2], T.nw[:, :].indirect(T.po[:, 0:8]), AF.Identity, bias=2048.0)], nwk, ["ouA"], dur=sd(128, GR))
    add("V", "un2", lambda: [V.tensor_scalar(T.ou[:, 1:256:2], T.nw[:, :].indirect(T.po[:, 8:16]), 2048.0, None, OP.add)], nwk, ["ouB"],
        dur=50 + vd(128, GR))

    def copies(eng, sem, cps, reads, key):
        def fn():
            return [V.tensor_copy(d, s) if eng == "V" else S.activation(d, s, AF.Copy) for d, s in cps]
        add(eng, sem, fn, reads, [key], dur=(vd(64) if eng == "V" else sd(64)) * len(cps), n=len(cps))
    blocks = [(T.sto[32 * a:32 * a + 32, 64 * q:64 * q + 64], T.ou[rows(q), 64 * a:64 * a + 64]) for q in others for a in range(4)]
    copies("V", "x0", blocks[:7], ["ouA", "ouB"], "stoV")
    copies("S", "sq0", blocks[7:], ["ouA", "ouB"], "stoS")
    s_o = send(["stoV", "stoS"], lambda q: T.sto[:, 64 * q:64 * q + 64], T.lr[:, 64 * r:64 * r + 64], "al%d" % r)
    add("Y", "dou", lambda: [g.sync.dma_start(T.yu[rows(r), :], T.ou[rows(r), :])], ["ouA", "ouB"], ["yu"], dur=100, lat=2000, inc=16)

    def back(j, q):
        arrive("al%d" % q, [q], "lr%d" % q, s_o, 3000.0 + 500.0 * j)
        cps = [(T.yo[rows(q), 64 * a:64 * a + 64], T.lr[32 * a:32 * a + 32, 64 * q:64 * q + 64]) for a in range(4)]
        m = 3 if j < 2 else 2
        copies("V", "x1", cps[:m], ["lr%d" % q], "yoV%d" % q)
        copies("S", "sq1", cps[m:], ["lr%d" % q], "yoS%d" % q)
        add("Y", "dou", lambda: [g.sync.dma_start(T.yu[rows(q), :], T.yo[rows(q), :])], ["yoV%d" % q, "yoS%d" % q], ["yu%d" % q], dur=100, lat=2000, inc=16)
    for j, q in enumerate(near + off):
        back(j, q)
    return emit(T, dict(V=V, S=S, P=P, G=g, Y=g.sync), tasks, count)


def place(tasks, pred, succ, key, back):
    n = len(tasks)
    need, st, busy = [len(p) for p in pred], [0.0] * n, {}
    pool = set(i for i in range(n) if need[i] == 0)
    while pool:
        i = min(pool, key=lambda j: (key[j], j))
        pool.discard(i)
        t = tasks[i]
        s, d = 0.0, t["dur"]
        for p, hard in pred[i]:
            s = max(s, st[p] + tasks[p]["dur"] + ((t if back else tasks[p])["lat"] + WAKE if hard else 0.0))
        if t["eng"] != "R":
            iv = busy.setdefault(t["eng"], [])
            j = len(iv)
            while j and iv[j - 1][1] > s:
                j -= 1
            while j < len(iv) and iv[j][0] < s + d - 0.001:
                s = max(s, iv[j][1])
                j += 1
            iv.insert(j, (s, s + d))
        st[i] = s
        for q, _ in succ[i]:
            need[q] -= 1
            if need[q] == 0:
                pool.add(q)
    return st


def bias(t):
    x = t["sem"]
    y = x.rstrip("0123456789")
    return SB.get(y, 0.0) + (LB * (3 - int(x[len(y):])) if y != x and len(y) <= 2 and y in LANE else 0.0)


def emit(T, E, tasks, count):
    n = len(tasks)
    pred, succ, before = [[] for _ in range(n)], [[] for _ in range(n)], {}
    for i, t in enumerate(tasks):
        if t["sem"] in before and tasks[before[t["sem"]]]["eng"] == t["eng"]:
            t["soft"].add(before[t["sem"]])
        before[t["sem"]] = i
        for hard, ds in ((1, t["deps"]), (0, t["soft"] - t["deps"])):
            for d in ds:
                pred[i].append((d, hard))
                succ[d].append((i, hard))
    rest = [0.0] * n
    for i in range(n - 1, -1, -1):
        rest[i] = tasks[i]["dur"] + tasks[i]["lat"] + max([rest[j] + WAKE for j, h in succ[i] if h] or [0.0])
    st = place(tasks, pred, succ, [-x - bias(t) for x, t in zip(rest, tasks)], False)
    best = (1e18, None)
    for k in range(ITERS + 1):
        end = max(s + t["dur"] + t["lat"] for s, t in zip(st, tasks))
        if end < best[0]:
            best = (end, st)
        if k < ITERS:
            sb = place(tasks, succ, pred, [-(s + t["dur"]) for s, t in zip(st, tasks)], True)
            st = place(tasks, pred, succ, [-(s + t["dur"]) for s, t in zip(sb, tasks)], False)
    st, seq = best[1], {}
    for i in sorted(range(n), key=lambda i: (st[i], i)):
        seq.setdefault(tasks[i]["eng"], []).append(i)
    clocks, after = {e: {} for e in E}, [None] * n
    pos, left = {e: 0 for e in seq}, n
    while left:
        was = left
        for e in seq:
            while pos[e] < len(seq[e]):
                i = seq[e][pos[e]]
                t = tasks[i]
                if any(after[d] is None for d in t["deps"]):
                    break
                ck = clocks.get(e, {})
                if e != "R":
                    for d in sorted(t["deps"], key=lambda d: -st[d]):
                        sem, val = tasks[d]["sem"], tasks[d]["val"]
                        if ck.get(sem, 0) < val:
                            E[e].wait_ge(T.sem[sem], int(val))
                            for s, v in after[d].items():
                                ck[s] = max(ck.get(s, 0), v)
                    for ins in t["fn"]():
                        ins.then_inc(T.sem[t["sem"]], t["inc"])
                after[i] = dict(ck)
                after[i][t["sem"]] = max(ck.get(t["sem"], 0), t["val"])
                pos[e] += 1
                left -= 1
        assert left < was
    last = {t["sem"]: s + t["dur"] + t["lat"] for s, t in zip(st, tasks)}
    for s in sorted(count, key=lambda s: (last[s], s)):
        E["P"].wait_ge(T.sem[s], int(count[s]))
    return seq, st, tasks
